import numpy as np
import ml_dtypes


def mxq(x, axis, fmt="e4m3"):
    dtype, down = {"e4m3": (ml_dtypes.float8_e4m3fn, 7), "e5m2": (ml_dtypes.float8_e5m2, 14)}[fmt]
    v = np.moveaxis(np.asarray(x, np.float32).astype(ml_dtypes.bfloat16).astype(np.float64), axis, -1)
    blocks = v.reshape(v.shape[:-1] + (-1, 32))
    amax = np.abs(blocks).max(-1, keepdims=True)
    byte = np.maximum(np.where(amax > 0, np.frexp(amax)[1] - 1 + 127, 0) - down, 1)
    scale = np.exp2(byte - 127.0)
    codes = (blocks / scale).astype(np.float32).astype(dtype).astype(np.float64)
    return np.moveaxis((codes * scale).reshape(v.shape), -1, axis)


WIDE = False


def mx_kscale(k):
    if not WIDE:
        return np.ones(k)
    levels = np.array([10, -10, 5, -5, 0])
    if k % 512:
        return np.exp2(np.random.permutation(np.resize(levels, k // 32))).repeat(32)
    a = np.empty((k // 512, 16))
    for p in range(k // 512):
        a[p, :8] = np.random.permutation(np.resize(levels, 8))
        for g in range(8):
            far = levels[np.abs(levels - a[p, g]) >= 10]
            a[p, g + 8] = far[np.random.randint(len(far))]
    return np.exp2(a.ravel()).repeat(32)


BF16 = ml_dtypes.bfloat16


def bf(x):
    return np.asarray(x, np.float32).astype(BF16)


def f64(x):
    return np.asarray(x).astype(np.float64)


E2M1 = np.array([0.0, 0.5, 1.0, 1.5, 2.0, 3.0, 4.0, 6.0, -0.0, -0.5, -1.0, -1.5, -2.0, -3.0, -4.0, -6.0])


def pack_weight(w, fmt):
    k, n = w.shape
    w = f64(bf(w)).reshape(k // 32, 32, n)
    amax = np.abs(w).max(1)
    if fmt == "e4m3":
        byte = np.frexp(amax)[1] - 1 + 127 - 7
    else:
        mant, ex = np.frexp(amax / 6.0)
        byte = np.where(mant > 0.5, ex, ex - 1) + 127
    byte = np.clip(np.where(amax > 0, byte, 1), 1, 254)
    scaled = (w * np.exp2(127.0 - byte)[:, None, :]).reshape(k, n).astype(np.float32)
    by_word = np.ascontiguousarray(scaled.reshape(k // 512, 128, 4, n).transpose(0, 1, 3, 2))
    if fmt == "e4m3":
        words = by_word.astype(ml_dtypes.float8_e4m3fn).view(np.uint8)
    else:
        c = by_word.astype(ml_dtypes.float4_e2m1fn).view(np.uint8) & 0xF
        words = c[..., 0::2] | (c[..., 1::2] << 4)
    return np.ascontiguousarray(words), np.ascontiguousarray(byte.astype(np.uint8).reshape(k // 512, 16, n))


def unpack_weight(words, scales, fmt):
    g, p, n, _ = words.shape
    if fmt == "e4m3":
        vals = np.ascontiguousarray(words).view(ml_dtypes.float8_e4m3fn).astype(np.float64)
    else:
        nib = np.empty((g, p, n, 4), np.uint8)
        nib[..., 0::2] = words & 0xF
        nib[..., 1::2] = words >> 4
        vals = E2M1[nib]
    vals = vals * np.repeat(np.exp2(scales.astype(np.float64) - 127.0), 8, axis=1)[..., None]
    return vals.transpose(0, 1, 3, 2).reshape(g * 512, n)
def pack4(w):
    words, scales = pack_weight(w, "e2m1")
    return words.reshape(words.shape[0], 128, -1), scales


def unpack4(words, scales):
    return unpack_weight(words.reshape(words.shape[0], 128, -1, 2), scales, "e2m1")


E4M3FN = np.array([(-1.0 if i & 128 else 1.0) * ((1.0 + (i & 7) / 8.0) * 2.0 ** (((i >> 3) & 15) - 7) if i & 120 else (i & 7) * 2.0 ** -9) for i in range(256)])


def e4m3fn_bytes(y):
    return np.clip(np.asarray(y, np.float64), -448.0, 448.0).astype(np.float32).astype(ml_dtypes.float8_e4m3fn).view(np.uint8)


def e4m3fn_values(b):
    return E4M3FN[b]

def planes(Y):
    n, m = Y.shape
    b = f64(bf(Y)).reshape(n // 32, 32, m)
    amax = np.abs(b).max(1)
    byte = np.clip(np.where(amax > 0, np.frexp(amax)[1] - 1 + 127 - 7, 1), 1, 254)
    codes = (b * np.exp2(127.0 - byte)[:, None, :]).reshape(n, m).astype(np.float32).astype(ml_dtypes.float8_e4m3fn).view(np.uint8)
    words = codes.reshape(n // 512, 128, 4, m).transpose(0, 1, 3, 2)
    return np.ascontiguousarray(words), np.ascontiguousarray(byte.astype(np.uint8).reshape(n // 512, 16, m))


T, K, F, L, N = 768, 1536, 1024, 512, 2048

def setup_inputs():
    s, t, r = mx_kscale(K), mx_kscale(F), mx_kscale(L)
    X = np.random.randn(K, T) * np.exp(0.3 * np.random.randn(K, 1)) * s[:, None]
    X_scale = (np.abs(X).max(axis=1, keepdims=True) / 448).astype(np.float32)
    X_bytes = e4m3fn_bytes(X / f64(X_scale))
    antenna = np.arange(K // 2)[:, None]
    u = np.random.uniform(-0.9, 0.9, (1, F))
    ph_a = np.pi * antenna * u
    ph_b = np.pi * antenna * (u + 8 / K)
    A = np.concatenate([np.cos(ph_a), np.sin(ph_a)], axis=0) * np.sqrt(2 / K)
    B = np.concatenate([np.cos(ph_b), np.sin(ph_b)], axis=0) * np.sqrt(2 / K)
    R = np.random.randn(F, L) * F ** -0.25 / np.sqrt(L)
    C_words, C_scales = pack4(np.random.randn(L, N) * r[:, None])
    return {"X_bytes": X_bytes, "X_scale": X_scale,
            "A": bf(A / s[:, None] * t[None, :]),
            "B": bf(B / s[:, None] * t[None, :]),
            "balance": bf(1 + 0.1 * np.random.randn(1, F)),
            "R": bf(R / t[:, None] / r[None, :]),
            "C_words": C_words, "C_scales": C_scales,
            "taper": bf(1 + 0.1 * np.random.randn(F, 1)),
            "gain": bf(np.exp(0.8 * np.random.randn(1, N)) * F ** -0.25),
            "offset": bf(0.3 * np.random.randn(1, N))}

def reference(X_bytes, X_scale, A, B, balance, R, C_words, C_scales, taper, gain, offset):
    X = e4m3fn_values(X_bytes) * f64(X_scale)
    Xq = mxq(X, 0, "e4m3")
    XA = Xq.T @ mxq(f64(A), 0, "e4m3")
    XB = Xq.T @ mxq(f64(B), 0, "e4m3")
    D = XA - f64(balance) * XB
    H = (mxq(f64(R), 1, "e4m3") @ unpack4(C_words, C_scales)) * f64(taper)
    Z = mxq(D, 1, "e4m3") @ mxq(H, 0, "e4m3")
    y = Z * f64(gain) + f64(offset)
    Y = y.T
    words, scales = planes(Y)
    return y, words, scales

@@ -1,0 +1,458 @@
+from contextlib import ExitStack
+
+import concourse.mybir as mybir
+from concourse.masks import make_identity
+
+T, K, F, L, N = 768, 1536, 1024, 512, 2048
+FLOPS = 2 * (2 * T * K * F + F * L * N + T * F * N)
+
+F32 = mybir.dt.float32
+BF16 = mybir.dt.bfloat16
+U32 = mybir.dt.uint32
+I32 = mybir.dt.int32
+U8 = mybir.dt.uint8
+FP8 = mybir.dt.float8_e4m3fn
+FP8X4 = mybir.dt.float8_e4m3fn_x4
+FP4X4 = mybir.dt.float4_e2m1fn_x4
+ALU = mybir.AluOpType
+ACT = mybir.ActivationFunctionType
+
+P = 128
+PACK = 4
+GROUP = P * PACK
+K_PASSES = K // GROUP
+F_GROUPS = F // GROUP
+N_GROUPS = N // GROUP
+PARTS = ((0, 512), (512, 256))
+
+
+def tile_squinted_beam_difference_codebook_b8_kernel(
+    tc, X_bytes, X_scale, A, B, balance, R, C_words, C_scales, taper, gain, offset, out_0, out_1, out_2
+):
+    nc = tc.nc
+    with ExitStack() as ctx:
+        keep = ctx.enter_context(tc.tile_pool(name="keep", bufs=1))
+        stage = ctx.enter_context(tc.tile_pool(name="stage", bufs=2))
+        psum = ctx.enter_context(tc.psum_pool(name="psum", bufs=8))
+        ctx.enter_context(tc.manual_schedule())
+
+        def new_bank():
+            return psum.tile([P, GROUP], F32, name="bank")
+
+        def copy_on(engine, out, in_):
+            if engine == "scalar":
+                nc.scalar.copy(out=out, in_=in_)
+            else:
+                nc.vector.tensor_copy(out=out, in_=in_)
+
+        def mx_tiles(name, width):
+            codes = keep.tile([P, width], U32, name=name + "_codes", align_bytes=64)
+            scales = keep.tile([P, width], U8, name=name + "_scales", align_bytes=64)
+            return codes, scales
+
+        def quantize(dst, col0, src):
+            cols = slice(col0, col0 + src.shape[1] // PACK)
+            nc.vector.quantize_mx(out=dst[0][:, cols].bitcast(FP8X4), scales=dst[1][:, cols], in_=src)
+
+        def grouped_tile():
+            return stage.tile([P, GROUP * PACK], BF16, name="grouped", bufs=8, align_bytes=64)
+
+        def matmul(out, lhs, lhs_cols, rhs, rhs_cols, start, stop):
+            nc.tensor.matmul_mx(
+                out=out,
+                lhsT=lhs[0][:, lhs_cols].bitcast(FP8X4),
+                lhsT_scale=lhs[1][:, lhs_cols],
+                rhs=rhs[0][:, rhs_cols].bitcast(FP8X4),
+                rhs_scale=rhs[1][:, rhs_cols],
+                start=start,
+                stop=stop,
+            )
+
+        def slot(t):
+            return slice(t * P, (t + 1) * P)
+
+        ident = keep.tile([P, P], F32, name="ident")
+        c_scales = keep.tile([P, N], U8, name="c_scales", align_bytes=64)
+        nc.gpsimd.memset(c_scales[:].bitcast(I32), 0)
+        make_identity(nc, ident[:])
+
+        banks_hbm = {"a": A, "b": B}
+        raw = {}
+        x_bytes = {}
+
+        def load_x(kp):
+            x_bytes[kp] = keep.tile([P, PACK, T], U8, name="x_bytes%d" % kp)
+            rows = X_bytes[kp * GROUP : (kp + 1) * GROUP, :]
+            nc.sync.dma_start(out=x_bytes[kp][:], in_=rows.rearrange("(p t) m -> p t m", t=PACK))
+
+        def load_bank(w, kp, fg):
+            raw[w, kp, fg] = stage.tile([P, PACK, GROUP], BF16, name="raw", bufs=8)
+            rows = banks_hbm[w][kp * GROUP : (kp + 1) * GROUP, fg * GROUP : (fg + 1) * GROUP]
+            nc.sync.dma_start(out=raw[w, kp, fg][:], in_=rows.rearrange("(p j) c -> p j c", j=PACK))
+
+        def load_r(fg):
+            raw["r", fg] = stage.tile([P, PACK, L], BF16, name="raw", bufs=8)
+            rows = R[fg * GROUP : (fg + 1) * GROUP, :]
+            nc.sync.dma_start(out=raw["r", fg][:], in_=rows.rearrange("(m t) l -> m t l", t=PACK))
+
+        def load_vector(name, hbm, groups):
+            v = keep.tile([P, groups, PACK], hbm.dtype, name=name)
+            nc.sync.dma_start(out=v[:], in_=hbm)
+            return v
+
+        def widen_vector(name, v):
+            wide = keep.tile(list(v.shape), F32, name=name)
+            nc.scalar.activation(out=wide[:], in_=v[:], func=ACT.Copy)
+            return wide
+
+        def load_c():
+            for q in range(4):
+                nc.sync.dma_start(
+                    out=c_scales[32 * q : 32 * q + 4, :].bitcast(I32), in_=C_scales[0, 4 * q : 4 * q + 4, :].bitcast(I32)
+                )
+            nc.sync.dma_start(out=c_words[:].bitcast(I32), in_=C_words[0].bitcast(I32))
+
+        c_words = keep.tile([P, 2 * N], U8, name="c_words", align_bytes=64)
+        balance16 = load_vector("balance16", balance.rearrange("o (g p t) -> p (o g) t", p=P, t=PACK), F_GROUPS)
+        load_bank("b", 0, 0)
+        x_scale = load_vector("x_scale", X_scale.rearrange("(g p t) o -> p g (t o)", p=P, t=PACK), K_PASSES)
+        load_x(0)
+        for kp in range(1, K_PASSES):
+            load_x(kp)
+            load_bank("b", kp, 0)
+        for kp in range(K_PASSES):
+            load_bank("a", kp, 0)
+        load_r(0)
+        load_r(1)
+        taper16 = load_vector("taper16", taper.rearrange("(g p t) o -> p g (t o)", p=P, t=PACK), F_GROUPS)
+        gain16 = load_vector("gain16", gain.rearrange("o (g p t) -> p (o g) t", p=P, t=PACK), N_GROUPS)
+        offset16 = load_vector("offset16", offset.rearrange("o (g p t) -> p (o g) t", p=P, t=PACK), N_GROUPS)
+
+        x_mx = [mx_tiles("x%d" % kp, T) for kp in range(K_PASSES)]
+        w_mx = {(w, kp, fg): mx_tiles("%s%d%d" % (w, kp, fg), GROUP) for w in "ab" for kp in range(K_PASSES) for fg in range(F_GROUPS)}
+        r_mx = [mx_tiles("r%d" % fg, GROUP) for fg in range(F_GROUPS)]
+        d_mx = {(fg, part): mx_tiles("d%d%d" % (fg, part), PARTS[part][1]) for fg in range(F_GROUPS) for part in range(2)}
+        h_mx = {(fg, ng): mx_tiles("h%d%d" % (fg, ng), GROUP) for fg in range(F_GROUPS) for ng in range(N_GROUPS)}
+        y_scales = keep.tile([P, N_GROUPS, T], U8, name="y_scales", align_bytes=64)
+        y_mx = [
+            (keep.tile([P, T], U32, name="y%d_codes" % ng, align_bytes=64), y_scales[:, ng, :]) for ng in range(N_GROUPS)
+        ]
+        x_planes, grouped, planes32 = {}, {}, {}
+
+        def widen_x(kp, engine):
+            x_planes[kp] = stage.tile([P, PACK, T], BF16, name="x_planes", bufs=3)
+            for t in range(PACK):
+                src = x_bytes[kp][:, t, :].bitcast(FP8)
+                if engine == "scalar":
+                    nc.scalar.activation(out=x_planes[kp][:, t, :], in_=src, func=ACT.Copy, scale=x_scale[:, kp, t : t + 1])
+                else:
+                    nc.vector.tensor_scalar(
+                        out=x_planes[kp][:, t, :], in0=src, scalar1=x_scale[:, kp, t : t + 1], scalar2=None, op0=ALU.mult
+                    )
+
+        def by_runs(planes):
+            return planes.rearrange("p t (c i) -> p c t i", i=4)
+
+        def grouped_by_runs(flat):
+            return flat.rearrange("p (c i t) -> p c t i", i=4, t=PACK)
+
+        def group_x(kp, part):
+            m0, width = PARTS[part]
+            grouped["x", kp, part] = grouped_tile()
+            nc.vector.tensor_copy(
+                out=grouped_by_runs(grouped["x", kp, part][:, : width * PACK]), in_=by_runs(x_planes[kp][:, :, m0 : m0 + width])
+            )
+
+        def quantize_x(kp, part):
+            m0, width = PARTS[part]
+            quantize(x_mx[kp], m0, grouped["x", kp, part][:, : width * PACK])
+
+        def group_bank(w, kp, fg, engine):
+            grouped[w, kp, fg] = grouped_tile()
+            copy_on(
+                engine,
+                grouped[w, kp, fg][:, : GROUP * PACK].rearrange("p (t m j) -> p m j t", t=PACK, j=PACK),
+                raw[w, kp, fg][:].rearrange("p j (m t) -> p m j t", t=PACK),
+            )
+
+        def quantize_bank(w, kp, fg):
+            quantize(w_mx[w, kp, fg], 0, grouped[w, kp, fg][:, : GROUP * PACK])
+
+        def wide_product(key, part, lhs_of_pass, rhs_of_pass, rhs_col0, passes, empty, pass_major=False):
+            width = PARTS[part][1]
+            planes32[key] = stage.tile([P, PACK, width], F32, name="planes32", bufs=4)
+            per_bank = GROUP // width
+            if pass_major:
+                banks = [new_bank() for t in range(PACK)]
+                for kp in range(passes):
+                    for t in range(PACK):
+                        matmul(banks[t][:, :width], lhs_of_pass(kp), slot(t), rhs_of_pass(kp),
+                               slice(rhs_col0, rhs_col0 + width), kp == 0, kp == passes - 1)
+                for t in range(PACK):
+                    empty(planes32[key][:, t, :], banks[t][:, :width], t)
+                return
+            for t0 in range(0, PACK, per_bank):
+                bank = new_bank()
+                for s in range(per_bank):
+                    for kp in range(passes):
+                        matmul(bank[:, s * width : (s + 1) * width], lhs_of_pass(kp), slot(t0 + s), rhs_of_pass(kp),
+                               slice(rhs_col0, rhs_col0 + width), kp == 0, kp == passes - 1)
+                for s in range(per_bank):
+                    empty(planes32[key][:, t0 + s, :], bank[:, s * width : (s + 1) * width], t0 + s)
+
+        def product_xb(fg, part, pass_major=False):
+            wide_product(
+                ("xb", fg, part), part, lambda kp: w_mx["b", kp, fg], lambda kp: x_mx[kp], PARTS[part][0], K_PASSES,
+                lambda out, in_, t: nc.scalar.activation(out=out, in_=in_, func=ACT.Copy, scale=balance32[:, fg, t : t + 1]),
+                pass_major,
+            )
+
+        def product_xa(fg, part, tile):
+            m0, width = PARTS[part]
+            if tile == 0:
+                grouped["d", fg, part] = grouped_tile()
+            bank = new_bank()
+            for t in range(PACK):
+                for kp in range(K_PASSES):
+                    matmul(bank[:, slot(t)], w_mx["a", kp, fg], slot(t), x_mx[kp],
+                           slice(m0 + tile * P, m0 + (tile + 1) * P), kp == 0, kp == K_PASSES - 1)
+            nc.vector.tensor_tensor(
+                out=grouped_by_runs(grouped["d", fg, part][:, tile * GROUP : (tile + 1) * GROUP]),
+                in0=by_runs(bank[:].rearrange("p (t m) -> p t m", t=PACK)),
+                in1=by_runs(planes32["xb", fg, part][:, :, slot(tile)]),
+                op=ALU.subtract,
+            )
+
+        def quantize_d(fg, part):
+            quantize(d_mx[fg, part], 0, grouped["d", fg, part][:, : PARTS[part][1] * PACK])
+
+        def turn_r(fg):
+            grouped["r", fg] = grouped_tile()
+            for t0 in range(0, PACK, 2):
+                bank = new_bank()
+                for s in range(2):
+                    words = raw["r", fg][:, t0 + s, :].bitcast(F32)
+                    for u in range(2):
+                        nc.tensor.transpose(bank[:, slot(2 * s + u)], words[:, u : L // 2 : 2], ident[:])
+                dst = grouped["r", fg][:, t0 * GROUP : (t0 + 2) * GROUP].bitcast(F32)
+                nc.scalar.copy(
+                    out=dst.rearrange("p (s m u) -> p s m u", s=2, u=2),
+                    in_=bank[:].rearrange("p (s u m) -> p s m u", s=2, u=2),
+                )
+
+        def quantize_r(fg):
+            quantize(r_mx[fg], 0, grouped["r", fg][:, : GROUP * PACK])
+
+        def product_h(fg, ng, quarter):
+            if quarter == 0:
+                grouped["h", fg, ng] = grouped_tile()
+            n0 = ng * GROUP + quarter * P
+            bank = new_bank()
+            for t in range(PACK):
+                nc.tensor.matmul_mx(
+                    out=bank[:, slot(t)],
+                    lhsT=r_mx[fg][0][:, slot(t)].bitcast(FP8X4),
+                    lhsT_scale=r_mx[fg][1][:, slot(t)],
+                    rhs=c_words[:, 2 * n0 : 2 * (n0 + P)].bitcast(FP4X4),
+                    rhs_scale=c_scales[:, n0 : n0 + P],
+                    start=True,
+                    stop=True,
+                )
+            dst = grouped["h", fg, ng][:, : GROUP * PACK].rearrange("p (tn m tf) -> p tn m tf", tn=PACK, tf=PACK)
+            nc.vector.tensor_tensor(
+                out=dst[:, :, quarter * 32 : (quarter + 1) * 32, :],
+                in0=bank[:].rearrange("p (tf m tn) -> p tn m tf", tf=PACK, tn=PACK),
+                in1=taper32[:, fg, :].unsqueeze(1).unsqueeze(1).to_broadcast([P, PACK, 32, PACK]),
+                op=ALU.mult,
+            )
+
+        def product_h_scalar(fg, ng, engine):
+            n0 = ng * GROUP
+            planes = stage.tile([P, PACK, GROUP], BF16, name="raw", bufs=8)
+            for t in range(PACK):
+                bank = new_bank()
+                nc.tensor.matmul_mx(
+                    out=bank[:],
+                    lhsT=r_mx[fg][0][:, slot(t)].bitcast(FP8X4),
+                    lhsT_scale=r_mx[fg][1][:, slot(t)],
+                    rhs=c_words[:, 2 * n0 : 2 * (n0 + GROUP)].bitcast(FP4X4),
+                    rhs_scale=c_scales[:, n0 : n0 + GROUP],
+                    start=True,
+                    stop=True,
+                )
+                nc.scalar.activation(
+                    out=planes[:, t, :].rearrange("p (tn m) -> p tn m", tn=PACK),
+                    in_=bank[:].rearrange("p (m tn) -> p tn m", tn=PACK),
+                    func=ACT.Copy,
+                    scale=taper32[:, fg, t : t + 1],
+                )
+            grouped["h", fg, ng] = grouped_tile()
+            copy_on(engine, grouped_by_runs(grouped["h", fg, ng][:]), by_runs(planes[:]))
+
+        def quantize_h(fg, ng):
+            quantize(h_mx[fg, ng], 0, grouped["h", fg, ng][:, : GROUP * PACK])
+
+        def product_z(ng, part, engine="scalar"):
+            def calibrate(out, in_, t):
+                gain_t, offset_t = gain32[:, ng, t : t + 1], offset32[:, ng, t : t + 1]
+                if engine == "scalar":
+                    nc.scalar.activation(out=out, in_=in_, func=ACT.Identity, scale=gain_t, bias=offset_t)
+                else:
+                    nc.vector.tensor_scalar(out=out, in0=in_, scalar1=gain_t, scalar2=offset_t, op0=ALU.mult, op1=ALU.add)
+
+            wide_product(("y", ng, part), part, lambda fg: h_mx[fg, ng], lambda fg: d_mx[fg, part], 0, F_GROUPS, calibrate)
+
+        def group_y(ng, part, engine="vector"):
+            width = PARTS[part][1]
+            grouped["y", ng, part] = grouped_tile()
+            copy_on(engine, grouped_by_runs(grouped["y", ng, part][:, : width * PACK]), by_runs(planes32["y", ng, part][:]))
+
+        def quantize_y(ng, part):
+            m0, width = PARTS[part]
+            quantize(y_mx[ng], m0, grouped["y", ng, part][:, : width * PACK])
+
+        def store_words(ng, part):
+            m0, width = PARTS[part]
+            words = out_1[ng, :, m0 : m0 + width, :].rearrange("p m t -> p (m t)")
+            nc.sync.dma_start(out=words.bitcast(I32), in_=y_mx[ng][0][:, m0 : m0 + width].bitcast(I32))
+
+        def store_scales():
+            for q in range(4):
+                rows = out_2[:, 4 * q : 4 * q + 4, :].bitcast(I32).rearrange("g r m -> r g m")
+                nc.sync.dma_start(out=rows, in_=y_scales[32 * q : 32 * q + 4, :, :].bitcast(I32))
+
+        def turn_y(ng, part, engines):
+            m0, width = PARTS[part]
+            for tile in range(width // P):
+                y_rows = stage.tile([P, GROUP], F32, name="y_rows", bufs=9)
+                bank = new_bank()
+                for t in range(PACK):
+                    nc.tensor.transpose(bank[:, slot(t)], planes32["y", ng, part][:, t, slot(tile)], ident[:])
+                copy_on(
+                    engines[tile % len(engines)],
+                    y_rows[:].rearrange("p (m t) -> p m t", t=PACK),
+                    bank[:].rearrange("p (t m) -> p m t", t=PACK),
+                )
+                tok0 = m0 + tile * P
+                nc.sync.dma_start(out=out_0[tok0 : tok0 + P, ng * GROUP : (ng + 1) * GROUP], in_=y_rows[:])
+
+        V, S = "vector", "scalar"
+        W, NARROW = 0, 1
+
+        def h_half(fg, ng):
+            for quarter in range(4):
+                product_h(fg, ng, quarter)
+
+        balance32 = widen_vector("balance32", balance16)
+        widen_x(0, S)
+        group_bank("b", 0, 0, V)
+        load_bank("b", 0, 1)
+        widen_x(1, S)
+        quantize_bank("b", 0, 0)
+        group_bank("b", 1, 0, V)
+        load_bank("b", 1, 1)
+        group_x(0, W)
+        quantize_bank("b", 1, 0)
+        widen_x(2, S)
+        group_x(0, NARROW)
+        quantize_x(0, W)
+        group_x(1, W)
+        quantize_x(0, NARROW)
+        group_bank("b", 2, 0, S)
+        load_bank("b", 2, 1)
+        load_c()
+        group_x(1, NARROW)
+        quantize_x(1, W)
+        group_x(2, W)
+        quantize_x(1, NARROW)
+        group_x(2, NARROW)
+        quantize_x(2, W)
+        quantize_bank("b", 2, 0)
+        group_bank("a", 0, 0, S)
+        load_bank("a", 0, 1)
+        product_xb(0, W, True)
+        quantize_x(2, NARROW)
+        group_bank("a", 1, 0, V)
+        load_bank("a", 1, 1)
+        group_bank("a", 2, 0, V)
+        load_bank("a", 2, 1)
+        quantize_bank("a", 1, 0)
+        quantize_bank("a", 0, 0)
+        product_xb(0, NARROW)
+        quantize_bank("a", 2, 0)
+        turn_r(0)
+        turn_r(1)
+        group_bank("b", 0, 1, V)
+        group_bank("b", 1, 1, V)
+        quantize_bank("b", 0, 1)
+        group_bank("b", 2, 1, S)
+        quantize_bank("b", 1, 1)
+        taper32 = widen_vector("taper32", taper16)
+        gain32 = widen_vector("gain32", gain16)
+        offset32 = widen_vector("offset32", offset16)
+        product_xa(0, W, 0)
+        quantize_r(0)
+        product_xa(0, W, 1)
+        quantize_bank("b", 2, 1)
+        group_bank("a", 0, 1, S)
+        product_xa(0, W, 2)
+        quantize_r(1)
+        product_xa(0, W, 3)
+        group_bank("a", 1, 1, V)
+        product_xa(0, NARROW, 0)
+        product_xa(0, NARROW, 1)
+        product_xb(1, W)
+        group_bank("a", 2, 1, V)
+        quantize_bank("a", 1, 1)
+        quantize_bank("a", 0, 1)
+        quantize_bank("a", 2, 1)
+        product_xb(1, NARROW)
+        quantize_d(0, W)
+        quantize_d(0, NARROW)
+        product_h_scalar(1, 0, S)
+        h_half(0, 0)
+        for tile in range(4):
+            product_xa(1, W, tile)
+            if tile == 0:
+                quantize_h(0, 0)
+        product_h_scalar(0, 1, S)
+        quantize_h(1, 0)
+        quantize_d(1, W)
+        product_xa(1, NARROW, 0)
+        product_xa(1, NARROW, 1)
+        last = N_GROUPS - 1
+        for ng in range(last):
+            product_z(ng, W)
+            if ng > 0:
+                group_y(ng - 1, NARROW, S)
+            h_half(1, ng + 1)
+            if ng == 0:
+                quantize_d(1, NARROW)
+            quantize_h(0, ng + 1)
+            if ng > 0:
+                quantize_y(ng - 1, NARROW)
+                turn_y(ng - 1, NARROW, [S])
+                store_words(ng - 1, NARROW)
+            group_y(ng, W)
+            turn_y(ng, W, [S])
+            quantize_h(1, ng + 1)
+            quantize_y(ng, W)
+            store_words(ng, W)
+            product_z(ng, NARROW)
+            if ng + 2 < N_GROUPS:
+                h_half(0, ng + 2)
+        product_z(last, W)
+        group_y(last - 1, NARROW)
+        turn_y(last - 1, NARROW, [V])
+        quantize_y(last - 1, NARROW)
+        store_words(last - 1, NARROW)
+        product_z(last, NARROW, V)
+        group_y(last, W)
+        turn_y(last, W, [S])
+        group_y(last, NARROW)
+        quantize_y(last, W)
+        store_words(last, W)
+        quantize_y(last, NARROW)
+        turn_y(last, NARROW, [S])
+        store_scales()
+        store_words(last, NARROW)

@@ -266,7 +266,7 @@ def tile_squinted_beam_difference_codebook_b8_kernel(
                 op=ALU.mult,
             )
 
-        def product_h_scalar(fg, ng, engine):
+        def product_h_scalar(fg, ng):
             n0 = ng * GROUP
             planes = stage.tile([P, PACK, GROUP], BF16, name="raw", bufs=8)
             for t in range(PACK):
@@ -286,8 +286,11 @@ def tile_squinted_beam_difference_codebook_b8_kernel(
                     func=ACT.Copy,
                     scale=taper32[:, fg, t : t + 1],
                 )
+            raw["h", fg, ng] = planes
+
+        def group_h(fg, ng, engine):
             grouped["h", fg, ng] = grouped_tile()
-            copy_on(engine, grouped_by_runs(grouped["h", fg, ng][:]), by_runs(planes[:]))
+            copy_on(engine, grouped_by_runs(grouped["h", fg, ng][:]), by_runs(raw["h", fg, ng][:]))
 
         def quantize_h(fg, ng):
             quantize(h_mx[fg, ng], 0, grouped["h", fg, ng][:, : GROUP * PACK])
@@ -316,10 +319,10 @@ def tile_squinted_beam_difference_codebook_b8_kernel(
             words = out_1[ng, :, m0 : m0 + width, :].rearrange("p m t -> p (m t)")
             nc.sync.dma_start(out=words.bitcast(I32), in_=y_mx[ng][0][:, m0 : m0 + width].bitcast(I32))
 
-        def store_scales():
+        def store_scales(groups):
             for q in range(4):
-                rows = out_2[:, 4 * q : 4 * q + 4, :].bitcast(I32).rearrange("g r m -> r g m")
-                nc.sync.dma_start(out=rows, in_=y_scales[32 * q : 32 * q + 4, :, :].bitcast(I32))
+                rows = out_2[groups, 4 * q : 4 * q + 4, :].bitcast(I32).rearrange("g r m -> r g m")
+                nc.sync.dma_start(out=rows, in_=y_scales[32 * q : 32 * q + 4, groups, :].bitcast(I32))
 
         def turn_y(ng, part, engines):
             m0, width = PARTS[part]
@@ -408,42 +411,49 @@ def tile_squinted_beam_difference_codebook_b8_kernel(
         quantize_bank("a", 2, 1)
         product_xb(1, NARROW)
         quantize_d(0, W)
-        quantize_d(0, NARROW)
-        product_h_scalar(1, 0, S)
+        product_h_scalar(1, 0)
+        group_h(1, 0, S)
         h_half(0, 0)
         for tile in range(4):
             product_xa(1, W, tile)
             if tile == 0:
                 quantize_h(0, 0)
-        product_h_scalar(0, 1, S)
+        product_h_scalar(0, 1)
         quantize_h(1, 0)
         quantize_d(1, W)
         product_xa(1, NARROW, 0)
         product_xa(1, NARROW, 1)
+        quantize_d(0, NARROW)
+        group_h(0, 1, V)
+        quantize_d(1, NARROW)
         last = N_GROUPS - 1
         for ng in range(last):
+            ahead = ng + 2 < N_GROUPS
             product_z(ng, W)
             if ng > 0:
                 group_y(ng - 1, NARROW, S)
             h_half(1, ng + 1)
-            if ng == 0:
-                quantize_d(1, NARROW)
             quantize_h(0, ng + 1)
             if ng > 0:
                 quantize_y(ng - 1, NARROW)
                 turn_y(ng - 1, NARROW, [S])
-                store_words(ng - 1, NARROW)
+            quantize_h(1, ng + 1)
             group_y(ng, W)
             turn_y(ng, W, [S])
-            quantize_h(1, ng + 1)
-            quantize_y(ng, W)
-            store_words(ng, W)
-            product_z(ng, NARROW)
-            if ng + 2 < N_GROUPS:
+            if ng > 0:
+                store_words(ng - 1, NARROW)
+            if ahead:
+                product_z(ng, NARROW, S)
                 h_half(0, ng + 2)
+                quantize_y(ng, W)
+            else:
+                product_z(ng, NARROW, V)
+                quantize_y(ng, W)
+            store_words(ng, W)
+        store_scales(slice(0, last - 1))
         product_z(last, W)
         group_y(last - 1, NARROW)
-        turn_y(last - 1, NARROW, [V])
+        turn_y(last - 1, NARROW, [S])
         quantize_y(last - 1, NARROW)
         store_words(last - 1, NARROW)
         product_z(last, NARROW, V)
@@ -454,5 +464,5 @@ def tile_squinted_beam_difference_codebook_b8_kernel(
         store_words(last, W)
         quantize_y(last, NARROW)
         turn_y(last, NARROW, [S])
-        store_scales()
         store_words(last, NARROW)
+        store_scales(slice(last - 1, N_GROUPS))

@@ -114,16 +114,14 @@ def tile_squinted_beam_difference_codebook_b8_kernel(
 
         c_words = keep.tile([P, 2 * N], U8, name="c_words", align_bytes=64)
         balance16 = load_vector("balance16", balance.rearrange("o (g p t) -> p (o g) t", p=P, t=PACK), F_GROUPS)
-        load_bank("b", 0, 0)
         x_scale = load_vector("x_scale", X_scale.rearrange("(g p t) o -> p g (t o)", p=P, t=PACK), K_PASSES)
-        load_x(0)
-        for kp in range(1, K_PASSES):
+        for kp in range(K_PASSES):
             load_x(kp)
             load_bank("b", kp, 0)
-        for kp in range(K_PASSES):
-            load_bank("a", kp, 0)
         load_r(0)
         load_r(1)
+        for kp in range(K_PASSES):
+            load_bank("a", kp, 0)
         taper16 = load_vector("taper16", taper.rearrange("(g p t) o -> p g (t o)", p=P, t=PACK), F_GROUPS)
         gain16 = load_vector("gain16", gain.rearrange("o (g p t) -> p (o g) t", p=P, t=PACK), N_GROUPS)
         offset16 = load_vector("offset16", offset.rearrange("o (g p t) -> p (o g) t", p=P, t=PACK), N_GROUPS)
@@ -137,24 +135,24 @@ def tile_squinted_beam_difference_codebook_b8_kernel(
         y_mx = [
             (keep.tile([P, T], U32, name="y%d_codes" % ng, align_bytes=64), y_scales[:, ng, :]) for ng in range(N_GROUPS)
         ]
-        x_planes, grouped, planes32 = {}, {}, {}
+        x_planes, grouped, planes32, r_banks = {}, {}, {}, {}
 
-        def widen_x(kp, engine):
+        def widen_x(kp, engines):
             x_planes[kp] = stage.tile([P, PACK, T], BF16, name="x_planes", bufs=3)
             for t in range(PACK):
                 src = x_bytes[kp][:, t, :].bitcast(FP8)
-                if engine == "scalar":
+                if engines[t] == "scalar":
                     nc.scalar.activation(out=x_planes[kp][:, t, :], in_=src, func=ACT.Copy, scale=x_scale[:, kp, t : t + 1])
                 else:
                     nc.vector.tensor_scalar(
                         out=x_planes[kp][:, t, :], in0=src, scalar1=x_scale[:, kp, t : t + 1], scalar2=None, op0=ALU.mult
                     )
 
-        def by_runs(planes):
-            return planes.rearrange("p t (c i) -> p c t i", i=4)
+        def by_runs(planes, run=4):
+            return planes.rearrange("p t (c i) -> p c t i", i=run)
 
-        def grouped_by_runs(flat):
-            return flat.rearrange("p (c i t) -> p c t i", i=4, t=PACK)
+        def grouped_by_runs(flat, run=4):
+            return flat.rearrange("p (c i t) -> p c t i", i=run, t=PACK)
 
         def group_x(kp, part):
             m0, width = PARTS[part]
@@ -178,8 +176,7 @@ def tile_squinted_beam_difference_codebook_b8_kernel(
         def quantize_bank(w, kp, fg):
             quantize(w_mx[w, kp, fg], 0, grouped[w, kp, fg][:, : GROUP * PACK])
 
-        def wide_product(key, part, lhs_of_pass, rhs_of_pass, rhs_col0, passes, empty, pass_major=False):
-            width = PARTS[part][1]
+        def wide_product(key, width, lhs_of_pass, rhs_of_pass, rhs_col0, passes, empty, pass_major=False):
             planes32[key] = stage.tile([P, PACK, width], F32, name="planes32", bufs=4)
             per_bank = GROUP // width
             if pass_major:
@@ -202,10 +199,19 @@ def tile_squinted_beam_difference_codebook_b8_kernel(
 
         def product_xb(fg, part, pass_major=False):
             wide_product(
-                ("xb", fg, part), part, lambda kp: w_mx["b", kp, fg], lambda kp: x_mx[kp], PARTS[part][0], K_PASSES,
+                ("xb", fg, part), PARTS[part][1], lambda kp: w_mx["b", kp, fg], lambda kp: x_mx[kp], PARTS[part][0], K_PASSES,
                 lambda out, in_, t: nc.scalar.activation(out=out, in_=in_, func=ACT.Copy, scale=balance32[:, fg, t : t + 1]),
                 pass_major,
             )
+
+        def xb_pass(banks, kp):
+            for t in range(PACK):
+                matmul(banks[t][:], w_mx["b", kp, 0], slot(t), x_mx[kp], slice(0, GROUP), kp == 0, kp == K_PASSES - 1)
+
+        def empty_xb(banks):
+            planes32["xb", 0, 0] = stage.tile([P, PACK, GROUP], F32, name="planes32", bufs=4)
+            for t in range(PACK):
+                nc.scalar.activation(out=planes32["xb", 0, 0][:, t, :], in_=banks[t][:], func=ACT.Copy, scale=balance32[:, 0, t : t + 1])
 
         def product_xa(fg, part, tile):
             m0, width = PARTS[part]
@@ -217,9 +223,9 @@ def tile_squinted_beam_difference_codebook_b8_kernel(
                     matmul(bank[:, slot(t)], w_mx["a", kp, fg], slot(t), x_mx[kp],
                            slice(m0 + tile * P, m0 + (tile + 1) * P), kp == 0, kp == K_PASSES - 1)
             nc.vector.tensor_tensor(
-                out=grouped_by_runs(grouped["d", fg, part][:, tile * GROUP : (tile + 1) * GROUP]),
-                in0=by_runs(bank[:].rearrange("p (t m) -> p t m", t=PACK)),
-                in1=by_runs(planes32["xb", fg, part][:, :, slot(tile)]),
+                out=grouped_by_runs(grouped["d", fg, part][:, tile * GROUP : (tile + 1) * GROUP], 2),
+                in0=by_runs(bank[:].rearrange("p (t m) -> p t m", t=PACK), 2),
+                in1=by_runs(planes32["xb", fg, part][:, :, slot(tile)], 2),
                 op=ALU.subtract,
             )
 
@@ -227,14 +233,16 @@ def tile_squinted_beam_difference_codebook_b8_kernel(
             quantize(d_mx[fg, part], 0, grouped["d", fg, part][:, : PARTS[part][1] * PACK])
 
         def turn_r(fg):
+            r_banks[fg] = [new_bank(), new_bank()]
+            for t in range(PACK):
+                words = raw["r", fg][:, t, :].bitcast(F32)
+                for u in range(2):
+                    nc.tensor.transpose(r_banks[fg][t // 2][:, slot(2 * (t % 2) + u)], words[:, u : L // 2 : 2], ident[:])
+
+        def group_r(fg):
             grouped["r", fg] = grouped_tile()
-            for t0 in range(0, PACK, 2):
-                bank = new_bank()
-                for s in range(2):
-                    words = raw["r", fg][:, t0 + s, :].bitcast(F32)
-                    for u in range(2):
-                        nc.tensor.transpose(bank[:, slot(2 * s + u)], words[:, u : L // 2 : 2], ident[:])
-                dst = grouped["r", fg][:, t0 * GROUP : (t0 + 2) * GROUP].bitcast(F32)
+            for half, bank in enumerate(r_banks[fg]):
+                dst = grouped["r", fg][:, 2 * half * GROUP : 2 * (half + 1) * GROUP].bitcast(F32)
                 nc.scalar.copy(
                     out=dst.rearrange("p (s m u) -> p s m u", s=2, u=2),
                     in_=bank[:].rearrange("p (s u m) -> p s m u", s=2, u=2),
@@ -295,27 +303,28 @@ def tile_squinted_beam_difference_codebook_b8_kernel(
         def quantize_h(fg, ng):
             quantize(h_mx[fg, ng], 0, grouped["h", fg, ng][:, : GROUP * PACK])
 
-        def product_z(ng, part, engine="scalar"):
+        def product_z(ng, span, engines):
+            m0, width = span
+            part = 0 if m0 < PARTS[1][0] else 1
+
             def calibrate(out, in_, t):
                 gain_t, offset_t = gain32[:, ng, t : t + 1], offset32[:, ng, t : t + 1]
-                if engine == "scalar":
+                if engines[t * len(engines) // PACK] == "scalar":
                     nc.scalar.activation(out=out, in_=in_, func=ACT.Identity, scale=gain_t, bias=offset_t)
                 else:
                     nc.vector.tensor_scalar(out=out, in0=in_, scalar1=gain_t, scalar2=offset_t, op0=ALU.mult, op1=ALU.add)
 
-            wide_product(("y", ng, part), part, lambda fg: h_mx[fg, ng], lambda fg: d_mx[fg, part], 0, F_GROUPS, calibrate)
+            wide_product(("y", ng, span), width, lambda fg: h_mx[fg, ng], lambda fg: d_mx[fg, part], m0 - PARTS[part][0], F_GROUPS, calibrate)
 
-        def group_y(ng, part, engine="vector"):
-            width = PARTS[part][1]
-            grouped["y", ng, part] = grouped_tile()
-            copy_on(engine, grouped_by_runs(grouped["y", ng, part][:, : width * PACK]), by_runs(planes32["y", ng, part][:]))
+        def group_y(ng, span, engine):
+            grouped["y", ng, span] = grouped_tile()
+            copy_on(engine, grouped_by_runs(grouped["y", ng, span][:, : span[1] * PACK], 2), by_runs(planes32["y", ng, span][:], 2))
 
-        def quantize_y(ng, part):
-            m0, width = PARTS[part]
-            quantize(y_mx[ng], m0, grouped["y", ng, part][:, : width * PACK])
+        def quantize_y(ng, span):
+            quantize(y_mx[ng], span[0], grouped["y", ng, span][:, : span[1] * PACK])
 
-        def store_words(ng, part):
-            m0, width = PARTS[part]
+        def store_words(ng, span):
+            m0, width = span
             words = out_1[ng, :, m0 : m0 + width, :].rearrange("p m t -> p (m t)")
             nc.sync.dma_start(out=words.bitcast(I32), in_=y_mx[ng][0][:, m0 : m0 + width].bitcast(I32))
 
@@ -324,13 +333,13 @@ def tile_squinted_beam_difference_codebook_b8_kernel(
                 rows = out_2[groups, 4 * q : 4 * q + 4, :].bitcast(I32).rearrange("g r m -> r g m")
                 nc.sync.dma_start(out=rows, in_=y_scales[32 * q : 32 * q + 4, groups, :].bitcast(I32))
 
-        def turn_y(ng, part, engines):
-            m0, width = PARTS[part]
+        def turn_y(ng, span, engines):
+            m0, width = span
             for tile in range(width // P):
                 y_rows = stage.tile([P, GROUP], F32, name="y_rows", bufs=9)
                 bank = new_bank()
                 for t in range(PACK):
-                    nc.tensor.transpose(bank[:, slot(t)], planes32["y", ng, part][:, t, slot(tile)], ident[:])
+                    nc.tensor.transpose(bank[:, slot(t)], planes32["y", ng, span][:, t, slot(tile)], ident[:])
                 copy_on(
                     engines[tile % len(engines)],
                     y_rows[:].rearrange("p (m t) -> p m t", t=PACK),
@@ -347,18 +356,22 @@ def tile_squinted_beam_difference_codebook_b8_kernel(
                 product_h(fg, ng, quarter)
 
         balance32 = widen_vector("balance32", balance16)
-        widen_x(0, S)
+        widen_x(0, [S, S, V, V])
         group_bank("b", 0, 0, V)
         load_bank("b", 0, 1)
-        widen_x(1, S)
+        widen_x(1, [S] * PACK)
+        group_x(0, W)
         quantize_bank("b", 0, 0)
         group_bank("b", 1, 0, V)
         load_bank("b", 1, 1)
-        group_x(0, W)
-        quantize_bank("b", 1, 0)
-        widen_x(2, S)
-        group_x(0, NARROW)
         quantize_x(0, W)
+        first_banks = [new_bank() for t in range(PACK)]
+        xb_pass(first_banks, 0)
+        turn_r(0)
+        turn_r(1)
+        group_x(0, NARROW)
+        quantize_bank("b", 1, 0)
+        widen_x(2, [S] * PACK)
         group_x(1, W)
         quantize_x(0, NARROW)
         group_bank("b", 2, 0, S)
@@ -366,25 +379,27 @@ def tile_squinted_beam_difference_codebook_b8_kernel(
         load_c()
         group_x(1, NARROW)
         quantize_x(1, W)
+        xb_pass(first_banks, 1)
         group_x(2, W)
         quantize_x(1, NARROW)
-        group_x(2, NARROW)
-        quantize_x(2, W)
         quantize_bank("b", 2, 0)
+        quantize_x(2, W)
+        xb_pass(first_banks, 2)
+        group_x(2, NARROW)
         group_bank("a", 0, 0, S)
         load_bank("a", 0, 1)
-        product_xb(0, W, True)
-        quantize_x(2, NARROW)
+        empty_xb(first_banks)
         group_bank("a", 1, 0, V)
         load_bank("a", 1, 1)
+        quantize_x(2, NARROW)
         group_bank("a", 2, 0, V)
         load_bank("a", 2, 1)
         quantize_bank("a", 1, 0)
         quantize_bank("a", 0, 0)
+        group_r(0)
+        group_r(1)
         product_xb(0, NARROW)
         quantize_bank("a", 2, 0)
-        turn_r(0)
-        turn_r(1)
         group_bank("b", 0, 1, V)
         group_bank("b", 1, 1, V)
         quantize_bank("b", 0, 1)
@@ -401,7 +416,7 @@ def tile_squinted_beam_difference_codebook_b8_kernel(
         product_xa(0, W, 2)
         quantize_r(1)
         product_xa(0, W, 3)
-        group_bank("a", 1, 1, V)
+        group_bank("a", 1, 1, S)
         product_xa(0, NARROW, 0)
         product_xa(0, NARROW, 1)
         product_xb(1, W)
@@ -427,42 +442,38 @@ def tile_squinted_beam_difference_codebook_b8_kernel(
         group_h(0, 1, V)
         quantize_d(1, NARROW)
         last = N_GROUPS - 1
+        wide, narrow = PARTS
         for ng in range(last):
             ahead = ng + 2 < N_GROUPS
-            product_z(ng, W)
+            product_z(ng, wide, [S])
             if ng > 0:
-                group_y(ng - 1, NARROW, S)
+                group_y(ng - 1, narrow, S)
             h_half(1, ng + 1)
             quantize_h(0, ng + 1)
             if ng > 0:
-                quantize_y(ng - 1, NARROW)
-                turn_y(ng - 1, NARROW, [S])
+                quantize_y(ng - 1, narrow)
+                turn_y(ng - 1, narrow, [S])
             quantize_h(1, ng + 1)
-            group_y(ng, W)
-            turn_y(ng, W, [S])
+            group_y(ng, wide, V)
+            turn_y(ng, wide, [S])
             if ng > 0:
-                store_words(ng - 1, NARROW)
+                store_words(ng - 1, narrow)
+            if not ahead:
+                store_scales(slice(0, last - 1))
+            product_z(ng, narrow, [S] if ahead else [S,V])
             if ahead:
-                product_z(ng, NARROW, S)
                 h_half(0, ng + 2)
-                quantize_y(ng, W)
-            else:
-                product_z(ng, NARROW, V)
-                quantize_y(ng, W)
-            store_words(ng, W)
-        store_scales(slice(0, last - 1))
-        product_z(last, W)
-        group_y(last - 1, NARROW)
-        turn_y(last - 1, NARROW, [S])
-        quantize_y(last - 1, NARROW)
-        store_words(last - 1, NARROW)
-        product_z(last, NARROW, V)
-        group_y(last, W)
-        turn_y(last, W, [S])
-        group_y(last, NARROW)
-        quantize_y(last, W)
-        store_words(last, W)
-        quantize_y(last, NARROW)
-        turn_y(last, NARROW, [S])
-        store_words(last, NARROW)
+            quantize_y(ng, wide)
+            store_words(ng, wide)
+        steps = [(last - 1, narrow)] + [(last, span) for span in ((0,256),(256,256),(512,256))]
+        group_y(*steps[0], V)
+        for i, step in enumerate(steps[:-1]):
+            product_z(*steps[i + 1], [S,V])
+            quantize_y(*step)
+            turn_y(*step, [S])
+            group_y(*steps[i + 1], V)
+            store_words(*step)
+        turn_y(*steps[-1], [V, S])
+        quantize_y(*steps[-1])
+        store_words(*steps[-1])
         store_scales(slice(last - 1, N_GROUPS))

@@ -23,7 +23,18 @@ GROUP = P * PACK
 K_PASSES = K // GROUP
 F_GROUPS = F // GROUP
 N_GROUPS = N // GROUP
-PARTS = ((0, 512), (512, 256))
+QUADRANTS = 4
+WIDE = (0, GROUP)
+NARROW = (GROUP, T - GROUP)
+LAST_SPANS = tuple((first, NARROW[1]) for first in range(0, T, NARROW[1]))
+RUN_BF16 = 4
+RUN_F32 = 2
+RAW_BUFS = 8
+GROUPED_BUFS = 7
+X_PLANES_BUFS = 3
+PLANES32_BUFS = 4
+Y_ROWS_BUFS = 7
+VECTOR, SCALAR = "vector", "scalar"
 
 
 def tile_squinted_beam_difference_codebook_b8_kernel(
@@ -39,23 +50,35 @@ def tile_squinted_beam_difference_codebook_b8_kernel(
         def new_bank():
             return psum.tile([P, GROUP], F32, name="bank")
 
-        def copy_on(engine, out, in_):
-            if engine == "scalar":
-                nc.scalar.copy(out=out, in_=in_)
-            else:
-                nc.vector.tensor_copy(out=out, in_=in_)
+        def raw_tile():
+            return stage.tile([P, PACK, GROUP], BF16, name="raw", bufs=RAW_BUFS)
+
+        def grouped_tile():
+            return stage.tile([P, GROUP * PACK], BF16, name="grouped", bufs=GROUPED_BUFS, align_bytes=64)
+
+        def handover_tile():
+            return stage.tile([P, GROUP * PACK], BF16, name="handover", bufs=1, align_bytes=64)
+
+        def planes32_tile(width):
+            return stage.tile([P, PACK, width], F32, name="planes32", bufs=PLANES32_BUFS)
 
         def mx_tiles(name, width):
             codes = keep.tile([P, width], U32, name=name + "_codes", align_bytes=64)
             scales = keep.tile([P, width], U8, name=name + "_scales", align_bytes=64)
             return codes, scales
 
+        def block(i):
+            return slice(i * P, (i + 1) * P)
+
+        def copy_on(engine, out, in_):
+            if engine == SCALAR:
+                nc.scalar.copy(out=out, in_=in_)
+            else:
+                nc.vector.tensor_copy(out=out, in_=in_)
+
         def quantize(dst, col0, src):
             cols = slice(col0, col0 + src.shape[1] // PACK)
             nc.vector.quantize_mx(out=dst[0][:, cols].bitcast(FP8X4), scales=dst[1][:, cols], in_=src)
-
-        def grouped_tile():
-            return stage.tile([P, GROUP * PACK], BF16, name="grouped", bufs=8, align_bytes=64)
 
         def matmul(out, lhs, lhs_cols, rhs, rhs_cols, start, stop):
             nc.tensor.matmul_mx(
@@ -68,15 +91,18 @@ def tile_squinted_beam_difference_codebook_b8_kernel(
                 stop=stop,
             )
 
-        def slot(t):
-            return slice(t * P, (t + 1) * P)
+        def planes_by_runs(planes, run):
+            return planes.rearrange("p t (c i) -> p c t i", i=run)
+
+        def grouped_by_runs(flat, run):
+            return flat.rearrange("p (c i t) -> p c t i", i=run, t=PACK)
 
         ident = keep.tile([P, P], F32, name="ident")
         c_scales = keep.tile([P, N], U8, name="c_scales", align_bytes=64)
         nc.gpsimd.memset(c_scales[:].bitcast(I32), 0)
         make_identity(nc, ident[:])
 
-        banks_hbm = {"a": A, "b": B}
+        steering = {"a": A, "b": B}
         raw = {}
         x_bytes = {}
 
@@ -85,13 +111,13 @@ def tile_squinted_beam_difference_codebook_b8_kernel(
             rows = X_bytes[kp * GROUP : (kp + 1) * GROUP, :]
             nc.sync.dma_start(out=x_bytes[kp][:], in_=rows.rearrange("(p t) m -> p t m", t=PACK))
 
-        def load_bank(w, kp, fg):
-            raw[w, kp, fg] = stage.tile([P, PACK, GROUP], BF16, name="raw", bufs=8)
-            rows = banks_hbm[w][kp * GROUP : (kp + 1) * GROUP, fg * GROUP : (fg + 1) * GROUP]
+        def load_steering(w, kp, fg):
+            raw[w, kp, fg] = raw_tile()
+            rows = steering[w][kp * GROUP : (kp + 1) * GROUP, fg * GROUP : (fg + 1) * GROUP]
             nc.sync.dma_start(out=raw[w, kp, fg][:], in_=rows.rearrange("(p j) c -> p j c", j=PACK))
 
         def load_r(fg):
-            raw["r", fg] = stage.tile([P, PACK, L], BF16, name="raw", bufs=8)
+            raw["r", fg] = raw_tile()
             rows = R[fg * GROUP : (fg + 1) * GROUP, :]
             nc.sync.dma_start(out=raw["r", fg][:], in_=rows.rearrange("(m t) l -> m t l", t=PACK))
 
@@ -106,7 +132,7 @@ def tile_squinted_beam_difference_codebook_b8_kernel(
             return wide
 
         def load_c():
-            for q in range(4):
+            for q in range(QUADRANTS):
                 nc.sync.dma_start(
                     out=c_scales[32 * q : 32 * q + 4, :].bitcast(I32), in_=C_scales[0, 4 * q : 4 * q + 4, :].bitcast(I32)
                 )
@@ -117,363 +143,397 @@ def tile_squinted_beam_difference_codebook_b8_kernel(
         x_scale = load_vector("x_scale", X_scale.rearrange("(g p t) o -> p g (t o)", p=P, t=PACK), K_PASSES)
         for kp in range(K_PASSES):
             load_x(kp)
-            load_bank("b", kp, 0)
-        load_r(0)
-        load_r(1)
+            load_steering("b", kp, 0)
+        for fg in range(F_GROUPS):
+            load_r(fg)
         for kp in range(K_PASSES):
-            load_bank("a", kp, 0)
+            load_steering("a", kp, 0)
         taper16 = load_vector("taper16", taper.rearrange("(g p t) o -> p g (t o)", p=P, t=PACK), F_GROUPS)
         gain16 = load_vector("gain16", gain.rearrange("o (g p t) -> p (o g) t", p=P, t=PACK), N_GROUPS)
         offset16 = load_vector("offset16", offset.rearrange("o (g p t) -> p (o g) t", p=P, t=PACK), N_GROUPS)
 
         x_mx = [mx_tiles("x%d" % kp, T) for kp in range(K_PASSES)]
-        w_mx = {(w, kp, fg): mx_tiles("%s%d%d" % (w, kp, fg), GROUP) for w in "ab" for kp in range(K_PASSES) for fg in range(F_GROUPS)}
+        w_mx = {
+            (w, kp, fg): mx_tiles("%s%d%d" % (w, kp, fg), GROUP)
+            for w in "ab"
+            for kp in range(K_PASSES)
+            for fg in range(F_GROUPS)
+        }
         r_mx = [mx_tiles("r%d" % fg, GROUP) for fg in range(F_GROUPS)]
-        d_mx = {(fg, part): mx_tiles("d%d%d" % (fg, part), PARTS[part][1]) for fg in range(F_GROUPS) for part in range(2)}
+        d_mx = {
+            (fg, span): mx_tiles("d%d%d" % (fg, i), span[1])
+            for fg in range(F_GROUPS)
+            for i, span in enumerate((WIDE, NARROW))
+        }
         h_mx = {(fg, ng): mx_tiles("h%d%d" % (fg, ng), GROUP) for fg in range(F_GROUPS) for ng in range(N_GROUPS)}
         y_scales = keep.tile([P, N_GROUPS, T], U8, name="y_scales", align_bytes=64)
         y_mx = [
             (keep.tile([P, T], U32, name="y%d_codes" % ng, align_bytes=64), y_scales[:, ng, :]) for ng in range(N_GROUPS)
         ]
-        x_planes, grouped, planes32, r_banks = {}, {}, {}, {}
+        x_planes, grouped, planes32, r_banks, xa_banks = {}, {}, {}, {}, {}
 
         def widen_x(kp, engines):
-            x_planes[kp] = stage.tile([P, PACK, T], BF16, name="x_planes", bufs=3)
+            x_planes[kp] = stage.tile([P, PACK, T], BF16, name="x_planes", bufs=X_PLANES_BUFS)
             for t in range(PACK):
                 src = x_bytes[kp][:, t, :].bitcast(FP8)
-                if engines[t] == "scalar":
+                if engines[t] == SCALAR:
                     nc.scalar.activation(out=x_planes[kp][:, t, :], in_=src, func=ACT.Copy, scale=x_scale[:, kp, t : t + 1])
                 else:
                     nc.vector.tensor_scalar(
                         out=x_planes[kp][:, t, :], in0=src, scalar1=x_scale[:, kp, t : t + 1], scalar2=None, op0=ALU.mult
                     )
 
-        def by_runs(planes, run=4):
-            return planes.rearrange("p t (c i) -> p c t i", i=run)
-
-        def grouped_by_runs(flat, run=4):
-            return flat.rearrange("p (c i t) -> p c t i", i=run, t=PACK)
-
-        def group_x(kp, part):
-            m0, width = PARTS[part]
-            grouped["x", kp, part] = grouped_tile()
+        def group_x(kp, span):
+            first, width = span
+            grouped["x", kp, span] = grouped_tile()
             nc.vector.tensor_copy(
-                out=grouped_by_runs(grouped["x", kp, part][:, : width * PACK]), in_=by_runs(x_planes[kp][:, :, m0 : m0 + width])
+                out=grouped_by_runs(grouped["x", kp, span][:, : width * PACK], RUN_BF16),
+                in_=planes_by_runs(x_planes[kp][:, :, first : first + width], RUN_BF16),
             )
 
-        def quantize_x(kp, part):
-            m0, width = PARTS[part]
-            quantize(x_mx[kp], m0, grouped["x", kp, part][:, : width * PACK])
+        def quantize_x(kp, span):
+            first, width = span
+            quantize(x_mx[kp], first, grouped["x", kp, span][:, : width * PACK])
 
-        def group_bank(w, kp, fg, engine):
+        def steering_views(w, kp, fg, order):
+            return (
+                grouped[w, kp, fg][:].rearrange("p (t m j) -> p " + order, t=PACK, j=PACK),
+                raw[w, kp, fg][:].rearrange("p j (m t) -> p " + order, t=PACK),
+            )
+
+        def group_steering(w, kp, fg, engine):
             grouped[w, kp, fg] = grouped_tile()
-            copy_on(
-                engine,
-                grouped[w, kp, fg][:, : GROUP * PACK].rearrange("p (t m j) -> p m j t", t=PACK, j=PACK),
-                raw[w, kp, fg][:].rearrange("p j (m t) -> p m j t", t=PACK),
-            )
+            copy_on(engine, *steering_views(w, kp, fg, "m j t"))
 
-        def quantize_bank(w, kp, fg):
-            quantize(w_mx[w, kp, fg], 0, grouped[w, kp, fg][:, : GROUP * PACK])
+        def group_steering_on_gpsimd(w, kp, fg):
+            grouped[w, kp, fg] = handover_tile()
+            dst, src = steering_views(w, kp, fg, "t m j")
+            nc.gpsimd.tensor_scalar(out=dst, in0=src, scalar1=1.0, scalar2=0.0, op0=ALU.mult, op1=ALU.add)
 
-        def wide_product(key, width, lhs_of_pass, rhs_of_pass, rhs_col0, passes, empty, pass_major=False):
-            planes32[key] = stage.tile([P, PACK, width], F32, name="planes32", bufs=4)
+        def quantize_steering(w, kp, fg):
+            quantize(w_mx[w, kp, fg], 0, grouped[w, kp, fg][:])
+
+        def group_a_half(kp, fg, half):
+            if half == 0:
+                grouped["a", kp, fg] = grouped_tile()
+            dst, src = steering_views("a", kp, fg, "m j t")
+            ts = slice(2 * half, 2 * half + 2)
+            nc.vector.tensor_copy(out=dst[:, :, :, ts], in_=src[:, :, :, ts])
+
+        def quantize_a_half(fg, half):
+            for kp in range(K_PASSES):
+                src = grouped["a", kp, fg][:, half * 2 * GROUP : (half + 1) * 2 * GROUP]
+                quantize(w_mx["a", kp, fg], half * 2 * P, src)
+
+        def product_to_planes(key, width, lhs_of_pass, rhs_of_pass, rhs_col0, passes, empty):
+            planes32[key] = planes32_tile(width)
             per_bank = GROUP // width
-            if pass_major:
-                banks = [new_bank() for t in range(PACK)]
-                for kp in range(passes):
-                    for t in range(PACK):
-                        matmul(banks[t][:, :width], lhs_of_pass(kp), slot(t), rhs_of_pass(kp),
-                               slice(rhs_col0, rhs_col0 + width), kp == 0, kp == passes - 1)
-                for t in range(PACK):
-                    empty(planes32[key][:, t, :], banks[t][:, :width], t)
-                return
+            rhs_cols = slice(rhs_col0, rhs_col0 + width)
             for t0 in range(0, PACK, per_bank):
                 bank = new_bank()
                 for s in range(per_bank):
-                    for kp in range(passes):
-                        matmul(bank[:, s * width : (s + 1) * width], lhs_of_pass(kp), slot(t0 + s), rhs_of_pass(kp),
-                               slice(rhs_col0, rhs_col0 + width), kp == 0, kp == passes - 1)
+                    out = bank[:, s * width : (s + 1) * width]
+                    for g in range(passes):
+                        matmul(out, lhs_of_pass(g), block(t0 + s), rhs_of_pass(g), rhs_cols, g == 0, g == passes - 1)
                 for s in range(per_bank):
                     empty(planes32[key][:, t0 + s, :], bank[:, s * width : (s + 1) * width], t0 + s)
 
-        def product_xb(fg, part, pass_major=False):
-            wide_product(
-                ("xb", fg, part), PARTS[part][1], lambda kp: w_mx["b", kp, fg], lambda kp: x_mx[kp], PARTS[part][0], K_PASSES,
-                lambda out, in_, t: nc.scalar.activation(out=out, in_=in_, func=ACT.Copy, scale=balance32[:, fg, t : t + 1]),
-                pass_major,
+        def balance_xb(out, in_, fg, t):
+            nc.scalar.activation(out=out, in_=in_, func=ACT.Copy, scale=balance32[:, fg, t : t + 1])
+
+        def product_xb(fg, span):
+            product_to_planes(
+                ("xb", fg, span),
+                span[1],
+                lambda kp: w_mx["b", kp, fg],
+                lambda kp: x_mx[kp],
+                span[0],
+                K_PASSES,
+                lambda out, in_, t: balance_xb(out, in_, fg, t),
             )
 
-        def xb_pass(banks, kp):
+        def first_xb_pass(banks, kp):
             for t in range(PACK):
-                matmul(banks[t][:], w_mx["b", kp, 0], slot(t), x_mx[kp], slice(0, GROUP), kp == 0, kp == K_PASSES - 1)
+                matmul(banks[t][:], w_mx["b", kp, 0], block(t), x_mx[kp], slice(0, GROUP), kp == 0, kp == K_PASSES - 1)
 
-        def empty_xb(banks):
-            planes32["xb", 0, 0] = stage.tile([P, PACK, GROUP], F32, name="planes32", bufs=4)
+        def empty_first_xb(banks):
+            planes32["xb", 0, WIDE] = planes32_tile(GROUP)
             for t in range(PACK):
-                nc.scalar.activation(out=planes32["xb", 0, 0][:, t, :], in_=banks[t][:], func=ACT.Copy, scale=balance32[:, 0, t : t + 1])
+                balance_xb(planes32["xb", 0, WIDE][:, t, :], banks[t][:], 0, t)
 
-        def product_xa(fg, part, tile):
-            m0, width = PARTS[part]
-            if tile == 0:
-                grouped["d", fg, part] = grouped_tile()
-            bank = new_bank()
-            for t in range(PACK):
+        def xa_half(fg, span, tile, half):
+            if half == 0:
+                xa_banks[fg, span, tile] = new_bank()
+            cols = slice(span[0] + tile * P, span[0] + (tile + 1) * P)
+            for t in (2 * half, 2 * half + 1):
+                out = xa_banks[fg, span, tile][:, block(t)]
                 for kp in range(K_PASSES):
-                    matmul(bank[:, slot(t)], w_mx["a", kp, fg], slot(t), x_mx[kp],
-                           slice(m0 + tile * P, m0 + (tile + 1) * P), kp == 0, kp == K_PASSES - 1)
+                    matmul(out, w_mx["a", kp, fg], block(t), x_mx[kp], cols, kp == 0, kp == K_PASSES - 1)
+
+        def finish_d(fg, span, tile):
+            xa_half(fg, span, tile, 1)
+            if tile == 0:
+                grouped["d", fg, span] = grouped_tile()
             nc.vector.tensor_tensor(
-                out=grouped_by_runs(grouped["d", fg, part][:, tile * GROUP : (tile + 1) * GROUP], 2),
-                in0=by_runs(bank[:].rearrange("p (t m) -> p t m", t=PACK), 2),
-                in1=by_runs(planes32["xb", fg, part][:, :, slot(tile)], 2),
+                out=grouped_by_runs(grouped["d", fg, span][:, tile * GROUP : (tile + 1) * GROUP], RUN_F32),
+                in0=planes_by_runs(xa_banks[fg, span, tile][:].rearrange("p (t m) -> p t m", t=PACK), RUN_F32),
+                in1=planes_by_runs(planes32["xb", fg, span][:, :, block(tile)], RUN_F32),
                 op=ALU.subtract,
             )
 
-        def quantize_d(fg, part):
-            quantize(d_mx[fg, part], 0, grouped["d", fg, part][:, : PARTS[part][1] * PACK])
+        def quantize_d(fg, span):
+            quantize(d_mx[fg, span], 0, grouped["d", fg, span][:, : span[1] * PACK])
 
-        def turn_r(fg):
+        def transpose_r(fg):
             r_banks[fg] = [new_bank(), new_bank()]
             for t in range(PACK):
                 words = raw["r", fg][:, t, :].bitcast(F32)
                 for u in range(2):
-                    nc.tensor.transpose(r_banks[fg][t // 2][:, slot(2 * (t % 2) + u)], words[:, u : L // 2 : 2], ident[:])
+                    nc.tensor.transpose(r_banks[fg][t // 2][:, block(2 * (t % 2) + u)], words[:, u : L // 2 : 2], ident[:])
 
-        def group_r(fg):
-            grouped["r", fg] = grouped_tile()
+        def group_r(fg, dst_tile):
+            grouped["r", fg] = dst_tile
             for half, bank in enumerate(r_banks[fg]):
-                dst = grouped["r", fg][:, 2 * half * GROUP : 2 * (half + 1) * GROUP].bitcast(F32)
+                dst = dst_tile[:, 2 * half * GROUP : 2 * (half + 1) * GROUP].bitcast(F32)
                 nc.scalar.copy(
                     out=dst.rearrange("p (s m u) -> p s m u", s=2, u=2),
                     in_=bank[:].rearrange("p (s u m) -> p s m u", s=2, u=2),
                 )
 
         def quantize_r(fg):
-            quantize(r_mx[fg], 0, grouped["r", fg][:, : GROUP * PACK])
+            quantize(r_mx[fg], 0, grouped["r", fg][:])
 
-        def product_h(fg, ng, quarter):
-            if quarter == 0:
-                grouped["h", fg, ng] = grouped_tile()
-            n0 = ng * GROUP + quarter * P
-            bank = new_bank()
-            for t in range(PACK):
-                nc.tensor.matmul_mx(
-                    out=bank[:, slot(t)],
-                    lhsT=r_mx[fg][0][:, slot(t)].bitcast(FP8X4),
-                    lhsT_scale=r_mx[fg][1][:, slot(t)],
-                    rhs=c_words[:, 2 * n0 : 2 * (n0 + P)].bitcast(FP4X4),
-                    rhs_scale=c_scales[:, n0 : n0 + P],
-                    start=True,
-                    stop=True,
-                )
-            dst = grouped["h", fg, ng][:, : GROUP * PACK].rearrange("p (tn m tf) -> p tn m tf", tn=PACK, tf=PACK)
-            nc.vector.tensor_tensor(
-                out=dst[:, :, quarter * 32 : (quarter + 1) * 32, :],
-                in0=bank[:].rearrange("p (tf m tn) -> p tn m tf", tf=PACK, tn=PACK),
-                in1=taper32[:, fg, :].unsqueeze(1).unsqueeze(1).to_broadcast([P, PACK, 32, PACK]),
-                op=ALU.mult,
+        def matmul_rc(out, fg, t, n0, width):
+            nc.tensor.matmul_mx(
+                out=out,
+                lhsT=r_mx[fg][0][:, block(t)].bitcast(FP8X4),
+                lhsT_scale=r_mx[fg][1][:, block(t)],
+                rhs=c_words[:, 2 * n0 : 2 * (n0 + width)].bitcast(FP4X4),
+                rhs_scale=c_scales[:, n0 : n0 + width],
+                start=True,
+                stop=True,
             )
 
-        def product_h_scalar(fg, ng):
-            n0 = ng * GROUP
-            planes = stage.tile([P, PACK, GROUP], BF16, name="raw", bufs=8)
-            for t in range(PACK):
+        def product_h_by_vector(fg, ng):
+            grouped["h", fg, ng] = grouped_tile()
+            dst = grouped["h", fg, ng][:].rearrange("p (tn m tf) -> p tn m tf", tn=PACK, tf=PACK)
+            m_count = P // PACK
+            for quarter in range(GROUP // P):
                 bank = new_bank()
-                nc.tensor.matmul_mx(
-                    out=bank[:],
-                    lhsT=r_mx[fg][0][:, slot(t)].bitcast(FP8X4),
-                    lhsT_scale=r_mx[fg][1][:, slot(t)],
-                    rhs=c_words[:, 2 * n0 : 2 * (n0 + GROUP)].bitcast(FP4X4),
-                    rhs_scale=c_scales[:, n0 : n0 + GROUP],
-                    start=True,
-                    stop=True,
+                for tf in range(PACK):
+                    matmul_rc(bank[:, block(tf)], fg, tf, ng * GROUP + quarter * P, P)
+                nc.vector.tensor_tensor(
+                    out=dst[:, :, quarter * m_count : (quarter + 1) * m_count, :],
+                    in0=bank[:].rearrange("p (tf m tn) -> p tn m tf", tf=PACK, tn=PACK),
+                    in1=taper32[:, fg, :].unsqueeze(1).unsqueeze(1).to_broadcast([P, PACK, m_count, PACK]),
+                    op=ALU.mult,
                 )
+
+        def product_h_by_scalar(fg, ng):
+            planes = raw_tile()
+            for tf in range(PACK):
+                bank = new_bank()
+                matmul_rc(bank[:], fg, tf, ng * GROUP, GROUP)
                 nc.scalar.activation(
-                    out=planes[:, t, :].rearrange("p (tn m) -> p tn m", tn=PACK),
+                    out=planes[:, tf, :].rearrange("p (tn m) -> p tn m", tn=PACK),
                     in_=bank[:].rearrange("p (m tn) -> p tn m", tn=PACK),
                     func=ACT.Copy,
-                    scale=taper32[:, fg, t : t + 1],
+                    scale=taper32[:, fg, tf : tf + 1],
                 )
             raw["h", fg, ng] = planes
 
         def group_h(fg, ng, engine):
             grouped["h", fg, ng] = grouped_tile()
-            copy_on(engine, grouped_by_runs(grouped["h", fg, ng][:]), by_runs(raw["h", fg, ng][:]))
+            copy_on(
+                engine, grouped_by_runs(grouped["h", fg, ng][:], RUN_BF16), planes_by_runs(raw["h", fg, ng][:], RUN_BF16)
+            )
 
         def quantize_h(fg, ng):
-            quantize(h_mx[fg, ng], 0, grouped["h", fg, ng][:, : GROUP * PACK])
+            quantize(h_mx[fg, ng], 0, grouped["h", fg, ng][:])
 
-        def product_z(ng, span, engines):
-            m0, width = span
-            part = 0 if m0 < PARTS[1][0] else 1
+        def product_y(ng, span, engines):
+            first, width = span
+            d_span = WIDE if first < NARROW[0] else NARROW
 
             def calibrate(out, in_, t):
                 gain_t, offset_t = gain32[:, ng, t : t + 1], offset32[:, ng, t : t + 1]
-                if engines[t * len(engines) // PACK] == "scalar":
+                if engines[t * len(engines) // PACK] == SCALAR:
                     nc.scalar.activation(out=out, in_=in_, func=ACT.Identity, scale=gain_t, bias=offset_t)
                 else:
                     nc.vector.tensor_scalar(out=out, in0=in_, scalar1=gain_t, scalar2=offset_t, op0=ALU.mult, op1=ALU.add)
 
-            wide_product(("y", ng, span), width, lambda fg: h_mx[fg, ng], lambda fg: d_mx[fg, part], m0 - PARTS[part][0], F_GROUPS, calibrate)
+            product_to_planes(
+                ("y", ng, span),
+                width,
+                lambda fg: h_mx[fg, ng],
+                lambda fg: d_mx[fg, d_span],
+                first - d_span[0],
+                F_GROUPS,
+                calibrate,
+            )
 
         def group_y(ng, span, engine):
             grouped["y", ng, span] = grouped_tile()
-            copy_on(engine, grouped_by_runs(grouped["y", ng, span][:, : span[1] * PACK], 2), by_runs(planes32["y", ng, span][:], 2))
+            copy_on(
+                engine,
+                grouped_by_runs(grouped["y", ng, span][:, : span[1] * PACK], RUN_F32),
+                planes_by_runs(planes32["y", ng, span][:], RUN_F32),
+            )
 
         def quantize_y(ng, span):
             quantize(y_mx[ng], span[0], grouped["y", ng, span][:, : span[1] * PACK])
 
-        def store_words(ng, span):
-            m0, width = span
-            words = out_1[ng, :, m0 : m0 + width, :].rearrange("p m t -> p (m t)")
-            nc.sync.dma_start(out=words.bitcast(I32), in_=y_mx[ng][0][:, m0 : m0 + width].bitcast(I32))
+        def store_codes(ng, span):
+            first, width = span
+            codes = out_1[ng, :, first : first + width, :].rearrange("p m t -> p (m t)")
+            nc.sync.dma_start(out=codes.bitcast(I32), in_=y_mx[ng][0][:, first : first + width].bitcast(I32))
 
         def store_scales(groups):
-            for q in range(4):
+            for q in range(QUADRANTS):
                 rows = out_2[groups, 4 * q : 4 * q + 4, :].bitcast(I32).rearrange("g r m -> r g m")
                 nc.sync.dma_start(out=rows, in_=y_scales[32 * q : 32 * q + 4, groups, :].bitcast(I32))
 
-        def turn_y(ng, span, engines):
-            m0, width = span
+        def store_y(ng, span, engines):
+            first, width = span
             for tile in range(width // P):
-                y_rows = stage.tile([P, GROUP], F32, name="y_rows", bufs=9)
+                y_rows = stage.tile([P, GROUP], F32, name="y_rows", bufs=Y_ROWS_BUFS)
                 bank = new_bank()
                 for t in range(PACK):
-                    nc.tensor.transpose(bank[:, slot(t)], planes32["y", ng, span][:, t, slot(tile)], ident[:])
+                    nc.tensor.transpose(bank[:, block(t)], planes32["y", ng, span][:, t, block(tile)], ident[:])
                 copy_on(
                     engines[tile % len(engines)],
                     y_rows[:].rearrange("p (m t) -> p m t", t=PACK),
                     bank[:].rearrange("p (t m) -> p m t", t=PACK),
                 )
-                tok0 = m0 + tile * P
-                nc.sync.dma_start(out=out_0[tok0 : tok0 + P, ng * GROUP : (ng + 1) * GROUP], in_=y_rows[:])
+                row0 = first + tile * P
+                nc.sync.dma_start(out=out_0[row0 : row0 + P, ng * GROUP : (ng + 1) * GROUP], in_=y_rows[:])
 
-        V, S = "vector", "scalar"
-        W, NARROW = 0, 1
-
-        def h_half(fg, ng):
-            for quarter in range(4):
-                product_h(fg, ng, quarter)
 
         balance32 = widen_vector("balance32", balance16)
-        widen_x(0, [S, S, V, V])
-        group_bank("b", 0, 0, V)
-        load_bank("b", 0, 1)
-        widen_x(1, [S] * PACK)
-        group_x(0, W)
-        quantize_bank("b", 0, 0)
-        group_bank("b", 1, 0, V)
-        load_bank("b", 1, 1)
-        quantize_x(0, W)
+        widen_x(0, [SCALAR, SCALAR, VECTOR, VECTOR])
+        group_steering("b", 0, 0, VECTOR)
+        load_steering("b", 0, 1)
+        widen_x(1, [SCALAR] * PACK)
+        group_x(0, WIDE)
+        quantize_steering("b", 0, 0)
+        group_steering("b", 1, 0, VECTOR)
+        load_steering("b", 1, 1)
+        quantize_x(0, WIDE)
         first_banks = [new_bank() for t in range(PACK)]
-        xb_pass(first_banks, 0)
-        turn_r(0)
-        turn_r(1)
+        first_xb_pass(first_banks, 0)
+        for fg in range(F_GROUPS):
+            transpose_r(fg)
         group_x(0, NARROW)
-        quantize_bank("b", 1, 0)
-        widen_x(2, [S] * PACK)
-        group_x(1, W)
+        quantize_steering("b", 1, 0)
+        widen_x(2, [SCALAR] * PACK)
+        group_x(1, WIDE)
         quantize_x(0, NARROW)
-        group_bank("b", 2, 0, S)
-        load_bank("b", 2, 1)
+        group_steering("b", 2, 0, SCALAR)
+        load_steering("b", 2, 1)
         load_c()
         group_x(1, NARROW)
-        quantize_x(1, W)
-        xb_pass(first_banks, 1)
-        group_x(2, W)
+        quantize_x(1, WIDE)
+        first_xb_pass(first_banks, 1)
+        group_x(2, WIDE)
         quantize_x(1, NARROW)
-        quantize_bank("b", 2, 0)
-        quantize_x(2, W)
-        xb_pass(first_banks, 2)
+        quantize_steering("b", 2, 0)
+        quantize_x(2, WIDE)
+        first_xb_pass(first_banks, 2)
         group_x(2, NARROW)
-        group_bank("a", 0, 0, S)
-        load_bank("a", 0, 1)
-        empty_xb(first_banks)
-        group_bank("a", 1, 0, V)
-        load_bank("a", 1, 1)
+
+        group_steering("a", 0, 0, SCALAR)
+        load_steering("a", 0, 1)
+        empty_first_xb(first_banks)
+        for kp in range(1, K_PASSES):
+            group_a_half(kp, 0, 0)
         quantize_x(2, NARROW)
-        group_bank("a", 2, 0, V)
-        load_bank("a", 2, 1)
-        quantize_bank("a", 1, 0)
-        quantize_bank("a", 0, 0)
-        group_r(0)
-        group_r(1)
+        quantize_a_half(0, 0)
+        for kp in range(1, K_PASSES):
+            group_a_half(kp, 0, 1)
+            load_steering("a", kp, 1)
+        group_r(0, handover_tile())
+        group_r(1, keep.tile([P, GROUP * PACK], BF16, name="r_grouped", align_bytes=64))
         product_xb(0, NARROW)
-        quantize_bank("a", 2, 0)
-        group_bank("b", 0, 1, V)
-        group_bank("b", 1, 1, V)
-        quantize_bank("b", 0, 1)
-        group_bank("b", 2, 1, S)
-        quantize_bank("b", 1, 1)
+        quantize_a_half(0, 1)
+        tiles = [(span, tile) for span in (WIDE, NARROW) for tile in range(span[1] // P)]
+        for span, tile in tiles:
+            xa_half(0, span, tile, 0)
+
+        group_steering("b", 0, 1, VECTOR)
+        group_steering("b", 1, 1, VECTOR)
+        quantize_steering("b", 0, 1)
+        group_steering("b", 2, 1, SCALAR)
+        quantize_steering("b", 1, 1)
+        quantize_steering("b", 2, 1)
+
+        quantize_r(0)
+        group_steering_on_gpsimd("a", 1, 1)
+        group_steering("a", 0, 1, SCALAR)
+        for span, tile in tiles:
+            finish_d(0, span, tile)
         taper32 = widen_vector("taper32", taper16)
+        product_xb(1, WIDE)
+        quantize_r(1)
+        for half in range(2):
+            group_a_half(2, 1, half)
+            quantize_a_half(1, half)
+        quantize_d(0, WIDE)
+        product_xb(1, NARROW)
         gain32 = widen_vector("gain32", gain16)
         offset32 = widen_vector("offset32", offset16)
-        product_xa(0, W, 0)
-        quantize_r(0)
-        product_xa(0, W, 1)
-        quantize_bank("b", 2, 1)
-        group_bank("a", 0, 1, S)
-        product_xa(0, W, 2)
-        quantize_r(1)
-        product_xa(0, W, 3)
-        group_bank("a", 1, 1, S)
-        product_xa(0, NARROW, 0)
-        product_xa(0, NARROW, 1)
-        product_xb(1, W)
-        group_bank("a", 2, 1, V)
-        quantize_bank("a", 1, 1)
-        quantize_bank("a", 0, 1)
-        quantize_bank("a", 2, 1)
-        product_xb(1, NARROW)
-        quantize_d(0, W)
-        product_h_scalar(1, 0)
-        group_h(1, 0, S)
-        h_half(0, 0)
-        for tile in range(4):
-            product_xa(1, W, tile)
-            if tile == 0:
-                quantize_h(0, 0)
-        product_h_scalar(0, 1)
+
+        product_h_by_scalar(0, 0)
+        group_h(0, 0, VECTOR)
+        product_h_by_scalar(1, 0)
+        group_h(1, 0, SCALAR)
+        for tile in range(WIDE[1] // P):
+            xa_half(1, WIDE, tile, 0)
+        for tile in range(WIDE[1] // P):
+            finish_d(1, WIDE, tile)
+        quantize_h(0, 0)
+        quantize_d(1, WIDE)
         quantize_h(1, 0)
-        quantize_d(1, W)
-        product_xa(1, NARROW, 0)
-        product_xa(1, NARROW, 1)
+        product_h_by_scalar(0, 1)
+        for tile in range(NARROW[1] // P):
+            xa_half(1, NARROW, tile, 0)
+            finish_d(1, NARROW, tile)
         quantize_d(0, NARROW)
-        group_h(0, 1, V)
+        group_h(0, 1, VECTOR)
         quantize_d(1, NARROW)
+
         last = N_GROUPS - 1
-        wide, narrow = PARTS
         for ng in range(last):
-            ahead = ng + 2 < N_GROUPS
-            product_z(ng, wide, [S])
+            more_h = ng + 2 < N_GROUPS
+            product_y(ng, WIDE, [SCALAR])
             if ng > 0:
-                group_y(ng - 1, narrow, S)
-            h_half(1, ng + 1)
+                group_y(ng - 1, NARROW, SCALAR)
+            product_h_by_vector(1, ng + 1)
             quantize_h(0, ng + 1)
             if ng > 0:
-                quantize_y(ng - 1, narrow)
-                turn_y(ng - 1, narrow, [S])
+                quantize_y(ng - 1, NARROW)
+                store_y(ng - 1, NARROW, [SCALAR])
             quantize_h(1, ng + 1)
-            group_y(ng, wide, V)
-            turn_y(ng, wide, [S])
+            group_y(ng, WIDE, VECTOR)
+            store_y(ng, WIDE, [SCALAR])
             if ng > 0:
-                store_words(ng - 1, narrow)
-            if not ahead:
-                store_scales(slice(0, last - 1))
-            product_z(ng, narrow, [S] if ahead else [S,V])
-            if ahead:
-                h_half(0, ng + 2)
-            quantize_y(ng, wide)
-            store_words(ng, wide)
-        steps = [(last - 1, narrow)] + [(last, span) for span in ((0,256),(256,256),(512,256))]
-        group_y(*steps[0], V)
-        for i, step in enumerate(steps[:-1]):
-            product_z(*steps[i + 1], [S,V])
+                store_codes(ng - 1, NARROW)
+            if not more_h:
+                store_scales(slice(0, ng))
+            product_y(ng, NARROW, [SCALAR] if more_h else [SCALAR, VECTOR])
+            if more_h:
+                product_h_by_vector(0, ng + 2)
+            quantize_y(ng, WIDE)
+            store_codes(ng, WIDE)
+
+        steps = [(last - 1, NARROW)] + [(last, span) for span in LAST_SPANS]
+        group_y(*steps[0], VECTOR)
+        for step, next_step in zip(steps, steps[1:]):
+            product_y(*next_step, [SCALAR, VECTOR])
             quantize_y(*step)
-            turn_y(*step, [S])
-            group_y(*steps[i + 1], V)
-            store_words(*step)
-        turn_y(*steps[-1], [V, S])
+            store_y(*step, [SCALAR])
+            group_y(*next_step, VECTOR)
+            store_codes(*step)
+        store_y(*steps[-1], [VECTOR, SCALAR])
         quantize_y(*steps[-1])
-        store_words(*steps[-1])
+        store_codes(*steps[-1])
         store_scales(slice(last - 1, N_GROUPS))

from contextlib import ExitStack

import concourse.mybir as mybir
from concourse.masks import make_identity

T, K, F, L, N = 768, 1536, 1024, 512, 2048
FLOPS = 2 * (2 * T * K * F + F * L * N + T * F * N)

F32 = mybir.dt.float32
BF16 = mybir.dt.bfloat16
U32 = mybir.dt.uint32
I32 = mybir.dt.int32
U8 = mybir.dt.uint8
FP8 = mybir.dt.float8_e4m3fn
FP8X4 = mybir.dt.float8_e4m3fn_x4
FP4X4 = mybir.dt.float4_e2m1fn_x4
ALU = mybir.AluOpType
ACT = mybir.ActivationFunctionType

P = 128
PACK = 4
GROUP = P * PACK
K_PASSES = K // GROUP
F_GROUPS = F // GROUP
N_GROUPS = N // GROUP
QUADRANTS = 4
WIDE = (0, GROUP)
NARROW = (GROUP, T - GROUP)
LAST_SPANS = tuple((first, NARROW[1]) for first in range(0, T, NARROW[1]))
RUN_BF16 = 4
RUN_F32 = 2
RAW_BUFS = 8
GROUPED_BUFS = 7
X_PLANES_BUFS = 3
PLANES32_BUFS = 4
Y_ROWS_BUFS = 7
VECTOR, SCALAR = "vector", "scalar"


def tile_squinted_beam_difference_codebook_b8_kernel(
    tc, X_bytes, X_scale, A, B, balance, R, C_words, C_scales, taper, gain, offset, out_0, out_1, out_2
):
    nc = tc.nc
    with ExitStack() as ctx:
        keep = ctx.enter_context(tc.tile_pool(name="keep", bufs=1))
        stage = ctx.enter_context(tc.tile_pool(name="stage", bufs=2))
        psum = ctx.enter_context(tc.psum_pool(name="psum", bufs=8))
        ctx.enter_context(tc.manual_schedule())

        def new_bank():
            return psum.tile([P, GROUP], F32, name="bank")

        def raw_tile():
            return stage.tile([P, PACK, GROUP], BF16, name="raw", bufs=RAW_BUFS)

        def grouped_tile():
            return stage.tile([P, GROUP * PACK], BF16, name="grouped", bufs=GROUPED_BUFS, align_bytes=64)

        def handover_tile():
            return stage.tile([P, GROUP * PACK], BF16, name="handover", bufs=1, align_bytes=64)

        def planes32_tile(width):
            return stage.tile([P, PACK, width], F32, name="planes32", bufs=PLANES32_BUFS)

        def mx_tiles(name, width):
            codes = keep.tile([P, width], U32, name=name + "_codes", align_bytes=64)
            scales = keep.tile([P, width], U8, name=name + "_scales", align_bytes=64)
            return codes, scales

        def block(i):
            return slice(i * P, (i + 1) * P)

        def copy_on(engine, out, in_):
            if engine == SCALAR:
                nc.scalar.copy(out=out, in_=in_)
            else:
                nc.vector.tensor_copy(out=out, in_=in_)

        def quantize(dst, col0, src):
            cols = slice(col0, col0 + src.shape[1] // PACK)
            nc.vector.quantize_mx(out=dst[0][:, cols].bitcast(FP8X4), scales=dst[1][:, cols], in_=src)

        def matmul(out, lhs, lhs_cols, rhs, rhs_cols, start, stop):
            nc.tensor.matmul_mx(
                out=out,
                lhsT=lhs[0][:, lhs_cols].bitcast(FP8X4),
                lhsT_scale=lhs[1][:, lhs_cols],
                rhs=rhs[0][:, rhs_cols].bitcast(FP8X4),
                rhs_scale=rhs[1][:, rhs_cols],
                start=start,
                stop=stop,
            )

        def planes_by_runs(planes, run):
            return planes.rearrange("p t (c i) -> p c t i", i=run)

        def grouped_by_runs(flat, run):
            return flat.rearrange("p (c i t) -> p c t i", i=run, t=PACK)

        ident = keep.tile([P, P], F32, name="ident")
        c_scales = keep.tile([P, N], U8, name="c_scales", align_bytes=64)
        nc.gpsimd.memset(c_scales[:].bitcast(I32), 0)
        make_identity(nc, ident[:])

        steering = {"a": A, "b": B}
        raw = {}
        x_bytes = {}

        def load_x(kp):
            x_bytes[kp] = keep.tile([P, PACK, T], U8, name="x_bytes%d" % kp)
            rows = X_bytes[kp * GROUP : (kp + 1) * GROUP, :]
            nc.sync.dma_start(out=x_bytes[kp][:], in_=rows.rearrange("(p t) m -> p t m", t=PACK))

        def load_steering(w, kp, fg):
            raw[w, kp, fg] = raw_tile()
            rows = steering[w][kp * GROUP : (kp + 1) * GROUP, fg * GROUP : (fg + 1) * GROUP]
            nc.sync.dma_start(out=raw[w, kp, fg][:], in_=rows.rearrange("(p j) c -> p j c", j=PACK))

        def load_r(fg):
            raw["r", fg] = raw_tile()
            rows = R[fg * GROUP : (fg + 1) * GROUP, :]
            nc.sync.dma_start(out=raw["r", fg][:], in_=rows.rearrange("(m t) l -> m t l", t=PACK))

        def load_vector(name, hbm, groups):
            v = keep.tile([P, groups, PACK], hbm.dtype, name=name)
            nc.sync.dma_start(out=v[:], in_=hbm)
            return v

        def widen_vector(name, v):
            wide = keep.tile(list(v.shape), F32, name=name)
            nc.scalar.activation(out=wide[:], in_=v[:], func=ACT.Copy)
            return wide

        def load_c():
            for q in range(QUADRANTS):
                nc.sync.dma_start(
                    out=c_scales[32 * q : 32 * q + 4, :].bitcast(I32), in_=C_scales[0, 4 * q : 4 * q + 4, :].bitcast(I32)
                )
            nc.sync.dma_start(out=c_words[:].bitcast(I32), in_=C_words[0].bitcast(I32))

        c_words = keep.tile([P, 2 * N], U8, name="c_words", align_bytes=64)
        balance16 = load_vector("balance16", balance.rearrange("o (g p t) -> p (o g) t", p=P, t=PACK), F_GROUPS)
        x_scale = load_vector("x_scale", X_scale.rearrange("(g p t) o -> p g (t o)", p=P, t=PACK), K_PASSES)
        for kp in range(K_PASSES):
            load_x(kp)
            load_steering("b", kp, 0)
        for fg in range(F_GROUPS):
            load_r(fg)
        for kp in range(K_PASSES):
            load_steering("a", kp, 0)
        taper16 = load_vector("taper16", taper.rearrange("(g p t) o -> p g (t o)", p=P, t=PACK), F_GROUPS)
        gain16 = load_vector("gain16", gain.rearrange("o (g p t) -> p (o g) t", p=P, t=PACK), N_GROUPS)
        offset16 = load_vector("offset16", offset.rearrange("o (g p t) -> p (o g) t", p=P, t=PACK), N_GROUPS)

        x_mx = [mx_tiles("x%d" % kp, T) for kp in range(K_PASSES)]
        w_mx = {
            (w, kp, fg): mx_tiles("%s%d%d" % (w, kp, fg), GROUP)
            for w in "ab"
            for kp in range(K_PASSES)
            for fg in range(F_GROUPS)
        }
        r_mx = [mx_tiles("r%d" % fg, GROUP) for fg in range(F_GROUPS)]
        d_mx = {
            (fg, span): mx_tiles("d%d%d" % (fg, i), span[1])
            for fg in range(F_GROUPS)
            for i, span in enumerate((WIDE, NARROW))
        }
        h_mx = {(fg, ng): mx_tiles("h%d%d" % (fg, ng), GROUP) for fg in range(F_GROUPS) for ng in range(N_GROUPS)}
        y_scales = keep.tile([P, N_GROUPS, T], U8, name="y_scales", align_bytes=64)
        y_mx = [
            (keep.tile([P, T], U32, name="y%d_codes" % ng, align_bytes=64), y_scales[:, ng, :]) for ng in range(N_GROUPS)
        ]
        x_planes, grouped, planes32, r_banks, xa_banks = {}, {}, {}, {}, {}

        def widen_x(kp, engines):
            x_planes[kp] = stage.tile([P, PACK, T], BF16, name="x_planes", bufs=X_PLANES_BUFS)
            for t in range(PACK):
                src = x_bytes[kp][:, t, :].bitcast(FP8)
                if engines[t] == SCALAR:
                    nc.scalar.activation(out=x_planes[kp][:, t, :], in_=src, func=ACT.Copy, scale=x_scale[:, kp, t : t + 1])
                else:
                    nc.vector.tensor_scalar(
                        out=x_planes[kp][:, t, :], in0=src, scalar1=x_scale[:, kp, t : t + 1], scalar2=None, op0=ALU.mult
                    )

        def group_x(kp, span):
            first, width = span
            grouped["x", kp, span] = grouped_tile()
            nc.vector.tensor_copy(
                out=grouped_by_runs(grouped["x", kp, span][:, : width * PACK], RUN_BF16),
                in_=planes_by_runs(x_planes[kp][:, :, first : first + width], RUN_BF16),
            )

        def quantize_x(kp, span):
            first, width = span
            quantize(x_mx[kp], first, grouped["x", kp, span][:, : width * PACK])

        def steering_views(w, kp, fg, order):
            return (
                grouped[w, kp, fg][:].rearrange("p (t m j) -> p " + order, t=PACK, j=PACK),
                raw[w, kp, fg][:].rearrange("p j (m t) -> p " + order, t=PACK),
            )

        def group_steering(w, kp, fg, engine):
            grouped[w, kp, fg] = grouped_tile()
            copy_on(engine, *steering_views(w, kp, fg, "m j t"))

        def group_steering_on_gpsimd(w, kp, fg):
            grouped[w, kp, fg] = handover_tile()
            dst, src = steering_views(w, kp, fg, "t m j")
            nc.gpsimd.tensor_scalar(out=dst, in0=src, scalar1=1.0, scalar2=0.0, op0=ALU.mult, op1=ALU.add)

        def quantize_steering(w, kp, fg):
            quantize(w_mx[w, kp, fg], 0, grouped[w, kp, fg][:])

        def group_a_half(kp, fg, half):
            if half == 0:
                grouped["a", kp, fg] = grouped_tile()
            dst, src = steering_views("a", kp, fg, "m j t")
            ts = slice(2 * half, 2 * half + 2)
            nc.vector.tensor_copy(out=dst[:, :, :, ts], in_=src[:, :, :, ts])

        def quantize_a_half(fg, half):
            for kp in range(K_PASSES):
                src = grouped["a", kp, fg][:, half * 2 * GROUP : (half + 1) * 2 * GROUP]
                quantize(w_mx["a", kp, fg], half * 2 * P, src)

        def product_to_planes(key, width, lhs_of_pass, rhs_of_pass, rhs_col0, passes, empty):
            planes32[key] = planes32_tile(width)
            per_bank = GROUP // width
            rhs_cols = slice(rhs_col0, rhs_col0 + width)
            for t0 in range(0, PACK, per_bank):
                bank = new_bank()
                for s in range(per_bank):
                    out = bank[:, s * width : (s + 1) * width]
                    for g in range(passes):
                        matmul(out, lhs_of_pass(g), block(t0 + s), rhs_of_pass(g), rhs_cols, g == 0, g == passes - 1)
                for s in range(per_bank):
                    empty(planes32[key][:, t0 + s, :], bank[:, s * width : (s + 1) * width], t0 + s)

        def balance_xb(out, in_, fg, t):
            nc.scalar.activation(out=out, in_=in_, func=ACT.Copy, scale=balance32[:, fg, t : t + 1])

        def product_xb(fg, span):
            product_to_planes(
                ("xb", fg, span),
                span[1],
                lambda kp: w_mx["b", kp, fg],
                lambda kp: x_mx[kp],
                span[0],
                K_PASSES,
                lambda out, in_, t: balance_xb(out, in_, fg, t),
            )

        def first_xb_pass(banks, kp):
            for t in range(PACK):
                matmul(banks[t][:], w_mx["b", kp, 0], block(t), x_mx[kp], slice(0, GROUP), kp == 0, kp == K_PASSES - 1)

        def empty_first_xb(banks):
            planes32["xb", 0, WIDE] = planes32_tile(GROUP)
            for t in range(PACK):
                balance_xb(planes32["xb", 0, WIDE][:, t, :], banks[t][:], 0, t)

        def xa_half(fg, span, tile, half):
            if half == 0:
                xa_banks[fg, span, tile] = new_bank()
            cols = slice(span[0] + tile * P, span[0] + (tile + 1) * P)
            for t in (2 * half, 2 * half + 1):
                out = xa_banks[fg, span, tile][:, block(t)]
                for kp in range(K_PASSES):
                    matmul(out, w_mx["a", kp, fg], block(t), x_mx[kp], cols, kp == 0, kp == K_PASSES - 1)

        def finish_d(fg, span, tile):
            xa_half(fg, span, tile, 1)
            if tile == 0:
                grouped["d", fg, span] = grouped_tile()
            nc.vector.tensor_tensor(
                out=grouped_by_runs(grouped["d", fg, span][:, tile * GROUP : (tile + 1) * GROUP], RUN_F32),
                in0=planes_by_runs(xa_banks[fg, span, tile][:].rearrange("p (t m) -> p t m", t=PACK), RUN_F32),
                in1=planes_by_runs(planes32["xb", fg, span][:, :, block(tile)], RUN_F32),
                op=ALU.subtract,
            )

        def quantize_d(fg, span):
            quantize(d_mx[fg, span], 0, grouped["d", fg, span][:, : span[1] * PACK])

        def transpose_r(fg):
            r_banks[fg] = [new_bank(), new_bank()]
            for t in range(PACK):
                words = raw["r", fg][:, t, :].bitcast(F32)
                for u in range(2):
                    nc.tensor.transpose(r_banks[fg][t // 2][:, block(2 * (t % 2) + u)], words[:, u : L // 2 : 2], ident[:])

        def group_r(fg, dst_tile):
            grouped["r", fg] = dst_tile
            for half, bank in enumerate(r_banks[fg]):
                dst = dst_tile[:, 2 * half * GROUP : 2 * (half + 1) * GROUP].bitcast(F32)
                nc.scalar.copy(
                    out=dst.rearrange("p (s m u) -> p s m u", s=2, u=2),
                    in_=bank[:].rearrange("p (s u m) -> p s m u", s=2, u=2),
                )

        def quantize_r(fg):
            quantize(r_mx[fg], 0, grouped["r", fg][:])

        def matmul_rc(out, fg, t, n0, width):
            nc.tensor.matmul_mx(
                out=out,
                lhsT=r_mx[fg][0][:, block(t)].bitcast(FP8X4),
                lhsT_scale=r_mx[fg][1][:, block(t)],
                rhs=c_words[:, 2 * n0 : 2 * (n0 + width)].bitcast(FP4X4),
                rhs_scale=c_scales[:, n0 : n0 + width],
                start=True,
                stop=True,
            )

        def product_h_by_vector(fg, ng):
            grouped["h", fg, ng] = grouped_tile()
            dst = grouped["h", fg, ng][:].rearrange("p (tn m tf) -> p tn m tf", tn=PACK, tf=PACK)
            m_count = P // PACK
            for quarter in range(GROUP // P):
                bank = new_bank()
                for tf in range(PACK):
                    matmul_rc(bank[:, block(tf)], fg, tf, ng * GROUP + quarter * P, P)
                nc.vector.tensor_tensor(
                    out=dst[:, :, quarter * m_count : (quarter + 1) * m_count, :],
                    in0=bank[:].rearrange("p (tf m tn) -> p tn m tf", tf=PACK, tn=PACK),
                    in1=taper32[:, fg, :].unsqueeze(1).unsqueeze(1).to_broadcast([P, PACK, m_count, PACK]),
                    op=ALU.mult,
                )

        def product_h_by_scalar(fg, ng):
            planes = raw_tile()
            for tf in range(PACK):
                bank = new_bank()
                matmul_rc(bank[:], fg, tf, ng * GROUP, GROUP)
                nc.scalar.activation(
                    out=planes[:, tf, :].rearrange("p (tn m) -> p tn m", tn=PACK),
                    in_=bank[:].rearrange("p (m tn) -> p tn m", tn=PACK),
                    func=ACT.Copy,
                    scale=taper32[:, fg, tf : tf + 1],
                )
            raw["h", fg, ng] = planes

        def group_h(fg, ng, engine):
            grouped["h", fg, ng] = grouped_tile()
            copy_on(
                engine, grouped_by_runs(grouped["h", fg, ng][:], RUN_BF16), planes_by_runs(raw["h", fg, ng][:], RUN_BF16)
            )

        def quantize_h(fg, ng):
            quantize(h_mx[fg, ng], 0, grouped["h", fg, ng][:])

        def product_y(ng, span, engines):
            first, width = span
            d_span = WIDE if first < NARROW[0] else NARROW

            def calibrate(out, in_, t):
                gain_t, offset_t = gain32[:, ng, t : t + 1], offset32[:, ng, t : t + 1]
                if engines[t * len(engines) // PACK] == SCALAR:
                    nc.scalar.activation(out=out, in_=in_, func=ACT.Identity, scale=gain_t, bias=offset_t)
                else:
                    nc.vector.tensor_scalar(out=out, in0=in_, scalar1=gain_t, scalar2=offset_t, op0=ALU.mult, op1=ALU.add)

            product_to_planes(
                ("y", ng, span),
                width,
                lambda fg: h_mx[fg, ng],
                lambda fg: d_mx[fg, d_span],
                first - d_span[0],
                F_GROUPS,
                calibrate,
            )

        def group_y(ng, span, engine):
            grouped["y", ng, span] = grouped_tile()
            copy_on(
                engine,
                grouped_by_runs(grouped["y", ng, span][:, : span[1] * PACK], RUN_F32),
                planes_by_runs(planes32["y", ng, span][:], RUN_F32),
            )

        def quantize_y(ng, span):
            quantize(y_mx[ng], span[0], grouped["y", ng, span][:, : span[1] * PACK])

        def store_codes(ng, span):
            first, width = span
            codes = out_1[ng, :, first : first + width, :].rearrange("p m t -> p (m t)")
            nc.sync.dma_start(out=codes.bitcast(I32), in_=y_mx[ng][0][:, first : first + width].bitcast(I32))

        def store_scales(groups):
            for q in range(QUADRANTS):
                rows = out_2[groups, 4 * q : 4 * q + 4, :].bitcast(I32).rearrange("g r m -> r g m")
                nc.sync.dma_start(out=rows, in_=y_scales[32 * q : 32 * q + 4, groups, :].bitcast(I32))

        def store_y(ng, span, engines):
            first, width = span
            for tile in range(width // P):
                y_rows = stage.tile([P, GROUP], F32, name="y_rows", bufs=Y_ROWS_BUFS)
                bank = new_bank()
                for t in range(PACK):
                    nc.tensor.transpose(bank[:, block(t)], planes32["y", ng, span][:, t, block(tile)], ident[:])
                copy_on(
                    engines[tile % len(engines)],
                    y_rows[:].rearrange("p (m t) -> p m t", t=PACK),
                    bank[:].rearrange("p (t m) -> p m t", t=PACK),
                )
                row0 = first + tile * P
                nc.sync.dma_start(out=out_0[row0 : row0 + P, ng * GROUP : (ng + 1) * GROUP], in_=y_rows[:])


        balance32 = widen_vector("balance32", balance16)
        widen_x(0, [SCALAR, SCALAR, VECTOR, VECTOR])
        group_steering("b", 0, 0, VECTOR)
        load_steering("b", 0, 1)
        widen_x(1, [SCALAR] * PACK)
        group_x(0, WIDE)
        quantize_steering("b", 0, 0)
        group_steering("b", 1, 0, VECTOR)
        load_steering("b", 1, 1)
        quantize_x(0, WIDE)
        first_banks = [new_bank() for t in range(PACK)]
        first_xb_pass(first_banks, 0)
        for fg in range(F_GROUPS):
            transpose_r(fg)
        group_x(0, NARROW)
        quantize_steering("b", 1, 0)
        widen_x(2, [SCALAR] * PACK)
        group_x(1, WIDE)
        quantize_x(0, NARROW)
        group_steering("b", 2, 0, SCALAR)
        load_steering("b", 2, 1)
        load_c()
        group_x(1, NARROW)
        quantize_x(1, WIDE)
        first_xb_pass(first_banks, 1)
        group_x(2, WIDE)
        quantize_x(1, NARROW)
        quantize_steering("b", 2, 0)
        quantize_x(2, WIDE)
        first_xb_pass(first_banks, 2)
        group_x(2, NARROW)

        group_steering("a", 0, 0, SCALAR)
        load_steering("a", 0, 1)
        empty_first_xb(first_banks)
        for kp in range(1, K_PASSES):
            group_a_half(kp, 0, 0)
        quantize_x(2, NARROW)
        quantize_a_half(0, 0)
        for kp in range(1, K_PASSES):
            group_a_half(kp, 0, 1)
            load_steering("a", kp, 1)
        group_r(0, handover_tile())
        group_r(1, keep.tile([P, GROUP * PACK], BF16, name="r_grouped", align_bytes=64))
        product_xb(0, NARROW)
        quantize_a_half(0, 1)
        tiles = [(span, tile) for span in (WIDE, NARROW) for tile in range(span[1] // P)]
        for span, tile in tiles:
            xa_half(0, span, tile, 0)

        group_steering("b", 0, 1, VECTOR)
        group_steering("b", 1, 1, VECTOR)
        quantize_steering("b", 0, 1)
        group_steering("b", 2, 1, SCALAR)
        quantize_steering("b", 1, 1)
        quantize_steering("b", 2, 1)

        quantize_r(0)
        group_steering_on_gpsimd("a", 1, 1)
        group_steering("a", 0, 1, SCALAR)
        for span, tile in tiles:
            finish_d(0, span, tile)
        taper32 = widen_vector("taper32", taper16)
        product_xb(1, WIDE)
        quantize_r(1)
        for half in range(2):
            group_a_half(2, 1, half)
            quantize_a_half(1, half)
        quantize_d(0, WIDE)
        product_xb(1, NARROW)
        gain32 = widen_vector("gain32", gain16)
        offset32 = widen_vector("offset32", offset16)

        product_h_by_scalar(0, 0)
        group_h(0, 0, VECTOR)
        product_h_by_scalar(1, 0)
        group_h(1, 0, SCALAR)
        for tile in range(WIDE[1] // P):
            xa_half(1, WIDE, tile, 0)
        for tile in range(WIDE[1] // P):
            finish_d(1, WIDE, tile)
        quantize_h(0, 0)
        quantize_d(1, WIDE)
        quantize_h(1, 0)
        product_h_by_scalar(0, 1)
        for tile in range(NARROW[1] // P):
            xa_half(1, NARROW, tile, 0)
            finish_d(1, NARROW, tile)
        quantize_d(0, NARROW)
        group_h(0, 1, VECTOR)
        quantize_d(1, NARROW)

        last = N_GROUPS - 1
        for ng in range(last):
            more_h = ng + 2 < N_GROUPS
            product_y(ng, WIDE, [SCALAR])
            if ng > 0:
                group_y(ng - 1, NARROW, SCALAR)
            product_h_by_vector(1, ng + 1)
            quantize_h(0, ng + 1)
            if ng > 0:
                quantize_y(ng - 1, NARROW)
                store_y(ng - 1, NARROW, [SCALAR])
            quantize_h(1, ng + 1)
            group_y(ng, WIDE, VECTOR)
            store_y(ng, WIDE, [SCALAR])
            if ng > 0:
                store_codes(ng - 1, NARROW)
            if not more_h:
                store_scales(slice(0, ng))
            product_y(ng, NARROW, [SCALAR] if more_h else [SCALAR, VECTOR])
            if more_h:
                product_h_by_vector(0, ng + 2)
            quantize_y(ng, WIDE)
            store_codes(ng, WIDE)

        steps = [(last - 1, NARROW)] + [(last, span) for span in LAST_SPANS]
        group_y(*steps[0], VECTOR)
        for step, next_step in zip(steps, steps[1:]):
            product_y(*next_step, [SCALAR, VECTOR])
            quantize_y(*step)
            store_y(*step, [SCALAR])
            group_y(*next_step, VECTOR)
            store_codes(*step)
        store_y(*steps[-1], [VECTOR, SCALAR])
        quantize_y(*steps[-1])
        store_codes(*steps[-1])
        store_scales(slice(last - 1, N_GROUPS))
